import numpy as np, ml_dtypes
CORES = [3,7,11,15,131,135,139,143]
N = 8
BF = ml_dtypes.bfloat16
S, L, CAP, RO, KM = 2048, 256, 48, 5, 3967
W = S + RO * CAP
def joined(c, T):
    e = np.add.accumulate(4 + (c & 3), axis=1)
    j = np.minimum(np.sum(e[:, :, None] <= (5 * np.arange(L) + 2)[None, None, :], axis=1), L - 2)
    p = np.take_along_axis(c, j, 1); q = np.take_along_axis(c, j + 1, 1)
    left = np.take_along_axis(T, p[:, None, :], 2)[:, 8:]; right = np.take_along_axis(T, q[:, None, :], 2)[:, :8]
    return p, np.concatenate([left, right], axis=1).astype(np.int64)
def places(z, w, k):
    u = np.sum(z * w[:, :, 0:1], axis=1) & (S - 1); v = np.sum(z * w[:, :, 1:2], axis=1) & (S - 1)
    return (((u * v) >> 5)[:, None, :] + k[:, :, None] * u[:, None, :]) & (S - 1)
def probe(z, w, k, b, U):
    h = places(z, w, k)
    d = np.stack([np.sum(np.abs(np.take_along_axis(U, h[:, m:m + 1], 2) - z), axis=1) for m in range(16)], axis=1)
    m = np.argmin(d, axis=1)[:, None, :]
    return np.take_along_axis(h, m, 1)[:, 0], np.take_along_axis(d, m, 1)[:, 0] < b[:, None]
def lowest(h, fit):
    win = np.zeros(fit.shape, bool)
    for g in range(8):
        i = np.flatnonzero(fit[g]); win[g, i[np.unique(h[g, i], return_index=True)[1]]] = True
    return win
def parts(rng):
    return (rng.integers(0, 256, (N, 8, 16, S), dtype=np.int16), rng.integers(0, 256, (N, 8, 16, S), dtype=np.int16), rng.integers(0, S, (N, 8, L)),
            rng.integers(0, 4096, (N, 8, 16, 2)), rng.integers(0, KM + 1, (N, 8, 16)), rng.integers(840, 1040, (N, 8)))
def pack(us, tp, c, w, k, th):
    return {"us": us.reshape(N, 128, S).astype(np.float32).astype(BF), "tp": tp.reshape(N, 128, S).astype(np.float32).astype(BF), "c0": np.ascontiguousarray(c).astype(np.int32),
            "hw": np.ascontiguousarray(w.reshape(N, 128, 2)).astype(np.int32), "km": np.ascontiguousarray(k.reshape(N, 128, 1)).astype(np.int32), "th": np.ascontiguousarray(th.reshape(N, 8, 1)).astype(np.int32)}
def setup_inputs(rng):
    return pack(*parts(rng))
def near(z, d):
    a = d[None, :] // 16 + (np.arange(16)[:, None] < d[None, :] % 16)
    return np.where(z < 128, z + a, z - a)
def setup_inputs_corners(rng):
    us, tp, c, w, k, th = parts(rng); w[:, :, 0, 0] |= 1; cnt = (0, 1, CAP - 1, CAP, CAP + 1, L); used = {}; sent = {}; zs = []
    def plant(q, g, h, z, todo):
        st, sl, ds = [], [], []
        for i, d in todo:
            r = int(rng.integers(0, 16)); cand = h[:, i].tolist()
            for m in range(16):
                s = cand[(m + r) % 16]
                if s not in used[q, g]:
                    used[q, g].add(s); st.append(s); sl.append(i); ds.append(d); break
        if st: us[q, g][:, np.array(st)] = near(z[:, np.array(sl)], np.array(ds))
    for q in range(N):
        for g in range(8):
            v = (g + q) % 8; used[q, g] = set()
            if v == 6: c[q, g] = 4 * rng.integers(0, S // 4, L) + 3; c[q, g, :3] = S - 1
            elif v == 7: c[q, g] = 4 * rng.integers(0, S // 4, L); c[q, g, L - 3:] = 0
            else: c[q, g] = 4 * rng.permutation(S // 4)[:L] + 1; k[q, g] = rng.permutation(min(S, KM + 1))[:16]; th[q, g] = rng.choice(np.array([1, 2, 64, 100]))
            if v in (1, 2, 3): us[q, g, :, 0] = 0; used[q, g].add(0)
        p, z = joined(c[q], tp[q]); even = (np.sum(z * w[q, :, :, 0:1], axis=1) & 1) == 0
        for g in range(8):
            if (g + q) % 8 < 6: tp[q, g, 8, np.unique(p[g, even[g]])] ^= 1
        p, z = joined(c[q], tp[q]); zs.append(z); h = places(z, w[q], k[q])
        for g in range(8):
            v = (g + q) % 8
            if v > 5: continue
            n = cnt[v]; pair = 2 if n >= 2 else 0; front = rng.permutation(L - 2).tolist(); t = int(th[q, g])
            poor = front[:n - pair] + ([L - 2, L - 1] if pair else []); fits = front[n - pair:] + ([] if pair else [L - 2])
            plant(q, g, h[g], z[g], [(i, (t - 1) * int(rng.integers(0, 2))) for i in fits] + [(i, t) for i in poor if i < L - 1 and rng.random() < 0.5])
            sent[q, g] = sorted(poor)[:CAP]
    for q in range(N):
        a = (q + 1) % N; h = places(zs[q], w[a], k[a])
        for g in range(8):
            if (q, g) in sent:
                t = int(th[a, g]); full = (g + q) % 8 == 4
                plant(a, g, h[g], zs[q][g], [(i, (0, t - 1, t)[int(rng.integers(0, 2 if full else 3))]) for i in sent[q, g] if i < L - 1 and (full or rng.random() < 0.6)])
    return pack(us, tp, c, w, k, th)
def setup_inputs_ends(rng):
    us = 255 * rng.integers(0, 2, (N, 8, 16, S), dtype=np.int16); tp = 255 * rng.integers(0, 2, (N, 8, 16, S), dtype=np.int16)
    inner = np.argsort(rng.random((N, 8, L)), axis=-1) < 5 * L // 16; anyc = rng.integers(0, S, (N, 8, L)); roll = rng.random((N, 8, L))
    w = 4095 * rng.integers(0, 2, (N, 8, 16, 2)); w[:, :, 0, 0] = 0; w[:, :, 1, 0] = 4095
    k = np.where(np.argsort(rng.random((N, 8, 16)), axis=-1) < 4, rng.integers(0, KM + 1, (N, 8, 16)), KM * rng.integers(0, 2, (N, 8, 16)))
    th = np.stack([4080 * (rng.permutation(8) % 2) for q in range(N)]); big = np.stack([rng.permutation(8) < 4 for q in range(N)]); big[:, 7] = True; big[0, 0] = True
    if th[N - 1, 7] == 0: th[N - 1, int(np.argmax(th[N - 1]))] = 0; th[N - 1, 7] = 4080
    c = np.where(inner, anyc, (S - 1) * (roll < 0.5)); base = ((S - 1) ** 2 >> 5) & (S - 1); one = np.zeros(16, np.int16); one[0] = 1
    for q in range(N):
        for g in range(8):
            if not big[q, g]: continue
            w[q, g] = 4095; us[q, g, :, 0] = 255; tp[q, g, :, 0] = 255; tp[q, g, :, S - 1] = 0; tp[q, g, :, S - 2] = 0; tp[q, g, 8, S - 2] = 1
            far = (S - 1, 1, 2) if g == 7 or rng.random() < 0.5 else (2, S - 1, 1)
            for lane, s in zip((1, 14, 15), far): k[q, g, lane] = (base - s) & (S - 1); us[q, g, :, s] = one
            k[q, g, 0] = 0; k[q, g, 2] = KM
            c[q, g] = np.where(inner[q, g], anyc[q, g] // 4 * 4, (S - 1) * (roll[q, g] < 0.2))
            if rng.random() < 0.5: c[q, g, 0] = S - 2; c[q, g, 1] = S - 1
            c[q, g, 4:6] = S - 1; c[q, g, 6:9] = 0; c[q, g, L - 2] = S - 2; c[q, g, L - 1] = S - 1
    return pack(us, tp, c, w, k, th)
def setup_inputs_refuse(rng):
    d = setup_inputs_ends(rng); d["th"][1] = 0
    return d
def setup_inputs_spread(rng):
    us, tp, c, w, k, th = parts(rng)
    def stones():
        v = np.floor(np.exp2(8 * rng.random((N, 8, 1, S), dtype=np.float32)) * rng.random((N, 8, 16, S), dtype=np.float32)).astype(np.int16)
        v = np.minimum(v, 255); return np.where(rng.random((N, 8, 1, S)) < 0.25, 255 - v, v)
    c = np.minimum((S * rng.random((N, 8, L)) ** 3).astype(np.int64), S - 1); c[:, ::2] = S - 1 - c[:, ::2]
    w = np.minimum(np.exp2(12.01 * rng.random((N, 8, 16, 2))).astype(np.int64) - (rng.random((N, 8, 16, 2)) < 0.05), 4095)
    k = np.maximum(np.minimum(np.exp2(12 * rng.random((N, 8, 16))).astype(np.int64) - 1, KM), 0)
    th = np.where(rng.random((N, 8)) < 0.25, rng.integers(0, 4081, (N, 8)), np.exp2(6 + 4 * rng.random((N, 8))).astype(np.int64))
    us = stones(); tp = stones()
    for q in range(N):
        g = int(rng.integers(0, 8))
        us[q, g] = rng.integers(0, 8, (16, S)); us[q, g, 0] += 248
        tp[q, g] = rng.integers(248, 256, (16, S)); tp[q, g, 8] = rng.integers(0, 2, S)
        w[q, g, :, 0] = 3072; w[q, g, 0, 0] = 4095; w[q, g, :, 1] = rng.integers(0, 4096, 16)
        k[q, g] = rng.permutation(KM + 1)[:16]; th[q, g] = 4080
    return pack(us, tp, c, w, k, th)
def setup_inputs_ties(rng):
    us, tp, c, w, k, th = parts(rng); flat = int(rng.integers(0, 8)); z = np.full((1, 16, 1), 255); z[0, 0] = 0
    for q in range(N):
        for g in range(8):
            pr = rng.integers(0, 256, (16, 12)); tp[q, g] = pr[:, rng.integers(0, 12, S)]
            us[q, g, :8] = pr[8:, rng.integers(0, 12, S)]; us[q, g, 8:] = pr[:8, rng.integers(0, 12, S)]
            th[q, g] = int(rng.choice(np.array([1, 400, 600, 700, 900])))
        us[q, flat] = 0; us[q, flat, 0] = 255; tp[q, flat] = 255; tp[q, flat, 8] = 0; th[q, flat] = 4080
        w[q, flat, 1, 0] ^= 1 - int(np.sum(w[q, flat, 1:, 0])) % 2
        if places(z, w[q, flat][None], k[q, flat][None])[0, 0, 0] == 0: k[q, flat, 0] ^= 1
    return pack(us, tp, c, w, k, th)
def check_inputs(d):
    bad = []
    for a, lo, hi in (("us", 0, 255), ("tp", 0, 255), ("c0", 0, S - 1), ("hw", 0, 4095), ("km", 0, KM), ("th", 0, 4080)):
        v = np.asarray(d[a]).astype(np.float64)
        if not (np.min(v) >= lo and np.max(v) <= hi): bad.append("range of " + a)
        elif np.any(v != np.floor(v)): bad.append("whole numbers in " + a)
    return bad
def reference(us, tp, c0, hw, km, th):
    U = np.zeros((N, 8, 16, W), np.int64); U[..., :S] = us.astype(np.float32).astype(np.int64).reshape(N, 8, 16, S)
    T = np.zeros((N, 8, 16, W), np.int64); T[..., :S] = tp.astype(np.float32).astype(np.int64).reshape(N, 8, 16, S)
    C = c0.astype(np.int64); w = hw.astype(np.int64).reshape(N, 8, 16, 2); k = km.astype(np.int64).reshape(N, 8, 16); t0 = th.astype(np.int64).reshape(N, 8)
    P = np.zeros(N, np.int64); out = []
    for t in range(RO):
        b = t0 + (P & 63)[:, None]; new, poor, zs = [], [], []
        for a in range(N):
            p, z = joined(C[a], T[a]); h, fit = probe(z, w[a], k[a], b[a], U[a]); win = lowest(h, fit)
            for g in range(8): U[a, g][:, h[g, win[g]]] = 255
            new.append(np.where(win, h, p)); poor.append(~fit); zs.append(z)
        for q in range(N):
            a = (q + 1 + t % (N - 1)) % N; sl = [np.flatnonzero(poor[q][g])[:CAP] for g in range(8)]
            z = np.zeros((8, 16, CAP), np.int64); use = np.zeros((8, CAP), bool)
            for g in range(8): z[g][:, :len(sl[g])] = zs[q][g][:, sl[g]]; use[g, :len(sl[g])] = True
            h, fit = probe(z, w[a], k[a], b[a], U[a]); win = lowest(h, fit & use)
            for g in range(8):
                s = np.flatnonzero(win[g]); n = h[g, s]; own = S + CAP * t + s
                U[q, g][:, own] = U[a, g][:, n]; T[q, g][:, own] = T[a, g][:, n]; U[a, g][:, n] = 255; new[q][g, sl[g][s]] = own
        P = np.array([int(np.sum(m)) for m in poor]); C = np.stack(new); out.append(C)
    return {"yc": np.concatenate(out, axis=2).astype(np.float32), "yu": U.reshape(N, 128, W).astype(np.float32).astype(BF)}

@@ -1,0 +1,560 @@
+from concourse.mybir import AluOpType as OP, ActivationFunctionType as AF
+
+RO, CAP, L, S = 5, 48, 256, 2048
+AREA = 560
+DL = S + 2 * AREA
+WID = DL + CAP
+ASKN = 800
+RETN = 104
+
+_sb = {
+    "U": (WID, "bfloat16"), "TW": (WID, "bfloat16"), "NW": (WID, "bfloat16"), "NH": (S, "bfloat16"),
+    "C0L": (16, "int32"), "HWI": (2, "int32"), "KMI": (1, "int32"), "THI": (1, "int32"),
+    "PIX": (1, "int32"), "PA_": (1, "int32"), "PG_": (1, "int32"), "COL": (16, "float32"), "SELC": (16, "float32"),
+    "GI": (128, "float32"), "YI": (144, "float32"), "AI": (256, "float32"),
+    "BO": (128, "bfloat16"), "BOH": (128, "float16"), "IDH": (128, "float16"), "SB": (144, "bfloat16"), "S16": (144, "bfloat16"), "SN": (144, "bfloat16"),
+    "S0": (144, "bfloat16"), "S256": (144, "bfloat16"), "SR": (2048, "bfloat16"), "PAM": (128, "bfloat16"), "PBM": (128, "bfloat16"),
+    "TRI": (128, "bfloat16"), "SHB": (128, "bfloat16"), "ONE": (128, "bfloat16"), "RST": (256, "float32"), "KEEP": (1024, "bfloat16"), "EA": (336, "float32"),
+    "MASK": (256, "bfloat16"), "DLP": (16, "float32"), "DLP32": (16, "float32"), "CL0": (16, "float32"),
+    "DC0": (16, "float32"), "DC1": (16, "float32"), "DC2": (16, "float32"), "DD0": (16, "float32"), "DD1": (16, "float32"),
+    "DD2": (16, "float32"), "FIXC": (16, "float32"), "FOUR": (16, "float32"),
+    "ZERO": (16, "float32"), "CI1": (256, "bfloat16"), "NB": (240, "bfloat16"), "C255": (256, "bfloat16"),
+    "S512": (48, "float32"), "E8": (128, "float32"), "THF": (16, "float32"), "TH16": (1, "float32"), "THR": (1, "float32"),
+    "WU": (16, "float16"), "WK": (128, "float16"), "WF": (2, "float32"), "WI": (2, "int32"), "KD": (16, "float16"), "KF": (1, "float32"),
+    "KI1": (1, "int32"), "KW": (16, "int32"), "KW2": (16, "int32"), "TMPC": (128, "float32"),
+    "ZB": (256, "bfloat16"), "UVI": (32, "int32"), "UVM": (32, "int32"), "TT": (16, "int32"), "TSI": (256, "int32"),
+    "BO300": (128, "float16"), "TXF": (256, "float16"), "HI": (256, "int32"), "HM": (256, "int32"), "H16": (256, "uint16"),
+    "ZS": (1536, "bfloat16"), "ZX": (4096, "bfloat16"), "DF": (4096, "bfloat16"), "KY": (256, "int32"),
+    "PQ": (16, "float32"), "XN": (16, "bfloat16"), "SC": (32, "bfloat16"), "SX": (16, "float32"), "E2": (16, "float32"), "PT": (32, "float32"),
+    "PU": (32, "float32"), "APL": (16, "uint16"), "ASKW": (ASKN, "bfloat16"), "PIN": (1, "int32"), "PI2": (1, "int32"),
+    "MC": (16, "int32"), "P32": (16, "float32"), "NE": (16, "float32"), "CODE": (16, "bfloat16"), "OH": (256, "float16"), "HO": (256, "float16"),
+    "HR": (256, "float16"), "M1": (256, "float32"), "LS": (256, "float32"), "EI": (256, "bfloat16"), "EB": (1920, "bfloat16"),
+    "EL": (16, "float32"), "HD": (16, "float32"), "HMM": (16, "float32"), "CM": (256, "float32"), "CS": (256, "float32"), "WA": (16, "float32"),
+    "WM": (16, "float32"), "LAY": (16, "uint16"), "LEN": (4, "uint16"),
+    "CI": (16, "int32"), "CW": (16, "int32"), "CE": (32, "bfloat16"), "CFI": (32, "int32"), "F1": (32, "bfloat16"),
+    "NN": (16, "bfloat16"), "NZ": (16, "float32"), "DZ": (16, "float32"), "PF": (16, "float32"), "JL": (16, "uint16"),
+    "J0": (ASKN, "bfloat16"), "JM": (256, "bfloat16"), "JF": (256, "bfloat16"), "SLOT": (16, "uint16"),
+    "F0R": (256, "float32"), "SLW": (ASKN, "float32"), "SLM": (48, "float32"), "SLS": (48, "float32"), "FIX": (4, "uint16"), "CF": (80, "float32"),
+    "ASKL": (RO * CAP, "bfloat16"), "RESP": (RETN, "bfloat16"), "RETL": (RO * RETN, "bfloat16"), "UB": (240, "bfloat16"),
+}
+_ps = ("pZ", "pUV", "pS", "pD", "pC", "pN", "pX", "pM")
+_place = {}
+_fill = {}
+for _k in _sb:
+    if _sb[_k][0] <= 48:
+        _d = _sb[_k][1]
+        _place[_k] = ("pack_" + _d, _fill.get(_d, 0))
+        _fill[_d] = _fill.get(_d, 0) + (_sb[_k][0] + 15) // 16 * 16
+SCRATCH = {k: ("sbuf", [128, _sb[k][0]], _sb[k][1]) for k in _sb if k not in _place}
+SCRATCH.update({"pack_" + k: ("sbuf", [128, _fill[k]], k) for k in _fill})
+SCRATCH.update({k: ("psum", [128, 512], "float32") for k in _ps})
+_bytes = {"bfloat16": 2, "float16": 2, "uint16": 2, "float32": 4, "int32": 4}
+SEMAPHORES = ["sV", "sA", "sP", "sG"] + ["d%d" % i for i in range(16)] + [a + str(t) for a in ("la", "lr", "aa", "ar") for t in range(RO)]
+CUTS = [(0, 64), (64, 96), (96, 160), (160, 208), (208, 240), (240, 256)]
+
+
+def rank_program(g, core, T, topo):
+    rank = T.rank_of(core)
+    if rank is None:
+        return
+    cores = list(T.cores)
+    N = len(cores)
+    Q = {"V": g.vector, "A": g.scalar, "P": g.tensor, "G": g, "S": g.sync}
+    count = {"sV": 0, "sA": 0, "sP": 0, "sG": 0}
+    know = {q: {} for q in Q}
+    snap = {}
+    hist = {}
+    ndma = [0]
+
+    def v(b, c0=0, c1=None, st=1, p=128, rows=None):
+        p = rows or p
+        if b in _place:
+            o = _place[b][1]
+            return (_place[b][0], o + c0, o + (_sb[b][0] if c1 is None else c1), st, p)
+        return (b, c0, (SCRATCH[b][1][1] if c1 is None else c1), st, p)
+
+    def ind(w, o):
+        return ("I", w, o)
+
+    def ap(x):
+        if x[0] == "I":
+            return ap(x[1]).indirect(ap(x[2]))
+        b, c0, c1, st, p = x
+        t = T[b]
+        if isinstance(p, tuple):
+            return t[p[0]:p[1]:p[2], c0:c1]
+        if st == 1:
+            return t[:, c0:c1] if p == 128 else t[0:p, c0:c1]
+        return t[:, c0:c1:st] if p == 128 else t[0:p, c0:c1:st]
+
+    def span(x):
+        n = _bytes[SCRATCH[x[0]][2]]
+        return x[0], x[1] * n // 16, (x[2] * n + 15) // 16
+
+    def learn(q, sem, val):
+        k = know[q]
+        if k.get(sem, 0) >= val:
+            return
+        k[sem] = val
+        for s2, v2 in snap.get((sem, val), {}).items():
+            if k.get(s2, 0) < v2:
+                k[s2] = v2
+
+    def need(q, rd, wr):
+        deps = {}
+        for x, w in [(x, False) for x in rd] + [(x, True) for x in wr]:
+            b, lo, hi = span(x)
+            ps = SCRATCH[b][0] == "psum"
+            keep = []
+            for e in hist.get(b, []):
+                elo, ehi, ew, eq, es, ev = e
+                hit = (ps and eq != q) or (not ps and elo < hi and lo < ehi)
+                if hit and (w or ew or ps):
+                    if deps.get(es, 0) < ev:
+                        deps[es] = ev
+                    if ps or (w and lo <= elo and ehi <= hi):
+                        continue
+                keep.append(e)
+            hist[b] = keep
+        for s in sorted(deps):
+            if know[q].get(s, 0) < deps[s]:
+                Q[q].wait_ge(T.sem[s], deps[s])
+                learn(q, s, deps[s])
+
+    def note(q, rd, wr, sem, val):
+        snap[(sem, val)] = dict(know[q])
+        for x, w in [(x, False) for x in rd] + [(x, True) for x in wr]:
+            b, lo, hi = span(x)
+            h = hist.setdefault(b, [])
+            h[:] = [e for e in h if not (e[0] == lo and e[1] == hi and e[2] == w and e[3] == q and e[4] == sem)]
+            h.append((lo, hi, w, q, sem, val))
+
+    def a_(x):
+        return ap(x) if isinstance(x, tuple) else x
+
+    def run(q, out, ins, f):
+        rd, wr = [], []
+        for x in ins:
+            if isinstance(x, tuple):
+                rd += [x[1], x[2]] if x[0] == "I" else [x]
+        if out[0] == "I":
+            wr.append(out[1])
+            rd.append(out[2])
+        else:
+            wr.append(out)
+        need(q, rd, wr)
+        s = "s" + q
+        count[s] += 1
+        f().then_inc(T.sem[s], 1)
+        note(q, rd, wr, s, count[s])
+
+    def cp(out, in_):
+        run("V", out, [in_], lambda: g.vector.tensor_copy(out=ap(out), in_=ap(in_)))
+
+    def tt(out, a, b, op):
+        run("V", out, [a, b], lambda: g.vector.tensor_tensor(out=ap(out), in0=ap(a), in1=ap(b), op=op))
+
+    def ts(out, a, s1, op0, s2=None, op1=None):
+        if op1 is None:
+            run("V", out, [a, s1], lambda: g.vector.tensor_scalar(out=ap(out), in0=ap(a), scalar1=a_(s1), scalar2=None, op0=op0))
+        else:
+            run("V", out, [a, s1, s2], lambda: g.vector.tensor_scalar(out=ap(out), in0=ap(a), scalar1=a_(s1), scalar2=a_(s2), op0=op0, op1=op1))
+
+    def scan(out, d0, d1, op0, op1):
+        run("V", out, [d0, d1], lambda: g.vector.tensor_tensor_scan(out=ap(out), data0=ap(d0), data1=ap(d1), initial=0.0, op0=op0, op1=op1))
+
+    def fill(out, c):
+        run("V", out, [], lambda: g.vector.memset(ap(out), c))
+
+    def act(out, in_, func=AF.Copy, scale=1.0, bias=0.0):
+        run("A", out, [in_, scale, bias], lambda: g.scalar.activation(out=ap(out), in_=ap(in_), func=func, bias=a_(bias), scale=a_(scale)))
+
+    def mm(out, lhsT, rhs, start=True, stop=True):
+        run("P", out, [lhsT, rhs], lambda: g.tensor.matmul(ap(out), ap(lhsT), ap(rhs), start=start, stop=stop))
+
+    def iota(out, pat, base=0, cm=0):
+        if SCRATCH[out[0]][2] != "int32":
+            run("G", out, [], lambda: g.iota(ap(out), pat, base, cm, allow_small_or_imprecise_dtypes=True))
+        else:
+            run("G", out, [], lambda: g.iota(ap(out), pat, base, cm))
+
+    def dma(q, out, in_):
+        rd = [in_] if isinstance(in_, tuple) else []
+        wr = [out] if isinstance(out, tuple) else []
+        need(q, rd, wr)
+        s = "d%d" % ndma[0]
+        ndma[0] += 1
+        Q[q].dma_start(out=a_(out), in_=a_(in_)).then_inc(T.sem[s], 16)
+        snap[(s, 16)] = dict(know[q])
+        for x, w in [(x, False) for x in rd] + [(x, True) for x in wr]:
+            b, lo, hi = span(x)
+            hist.setdefault(b, []).append((lo, hi, w, "dma", s, 16))
+
+    def engs(src, dst):
+        return topo.engines(src, dst)[:8]
+
+    def send(dst, out, in_, rsem, lsem):
+        need("G", [in_], [])
+        mask = 0
+        for e in engs(core, dst):
+            mask |= 1 << e
+        rid, pid = topo.addr(dst, core)
+        g.remote_dma(ap(out), ap(in_), T.sem[rsem], T.sem[lsem], pid, rid, mask)
+        b, lo, hi = span(in_)
+        hist.setdefault(b, []).append((lo, hi, False, "rdma", lsem, len(engs(core, dst))))
+        snap[(lsem, len(engs(core, dst)))] = dict(know["G"])
+
+    def arrives(x, src, rsem):
+        b, lo, hi = span(x)
+        hist.setdefault(b, []).append((lo, hi, True, "rdma", rsem, len(engs(src, core))))
+
+    dma("S", v("C0L"), T.c0[:])
+    dma("S", v("TW", 0, S), T.tp[:])
+    dma("A", v("HWI"), T.hw[:])
+    dma("A", v("KMI"), T.km[:])
+    dma("A", v("THI", p=8), T.th[:])
+    dma("A", v("U", 0, S), T.us[:])
+    iota(v("PIX"), [[0, 1]], 0, 1)
+    iota(v("GI"), [[1, 8], [0, 16]])
+    iota(v("AI"), [[0, 16], [1, 16]])
+    iota(v("YI"), [[1, 144]])
+    iota(v("CL0"), [[16, 16]])
+    iota(v("NW", 0, S), [[0, 128], [1, 16]])
+    iota(v("NH"), [[1, 128], [0, 16]])
+    dma("S", v("NW", 0, S, rows=(0, 128, 16)), v("NH", 0, S, rows=(0, 8, 1)))
+    iota(v("CI1"), [[1, 256]], 1)
+    iota(v("S512"), [[1, 48]], 256)
+    iota(v("NB"), [[0, 15], [1, 16]])
+    iota(v("NH", 0, 240), [[1, 15], [0, 16]], 128)
+    dma("S", v("NB", rows=(0, 128, 16)), v("NH", 0, 240, rows=(0, 8, 1)))
+    PIX, PA, PG = v("PIX"), v("PA_"), v("PG_")
+
+    def col(i):
+        return v("COL", i, i + 1)
+    ts(PA, PIX, 15, OP.bitwise_and)
+    ts(PG, PIX, 4, OP.arith_shift_right)
+    cp(col(0), PA)
+    cp(col(1), PG)
+    cp(col(3), PIX)
+    GI, YI = v("GI"), v("YI", 0, 128)
+    ts(v("BO"), GI, col(1), OP.is_equal)
+    ts(v("SELC"), v("AI", 0, 16), col(0), OP.is_equal)
+    for j in range(4):
+        act(v("KEEP", 256 * j, 256 * j + 256), v("AI"), AF.Sign)
+    act(v("ZS", 0, 1024), v("KEEP"), scale=0.0)
+    act(v("ZS", 1024, 1536), v("KEEP", 0, 512), scale=0.0)
+    ts(PA, PIX, 4, OP.arith_shift_right)
+    ts(PG, PA, 1, OP.bitwise_and)
+    cp(col(6), PG)
+    ts(col(5), col(6), -1.0, OP.mult, 1.0, OP.add)
+    cp(v("BOH"), v("BO"))
+    ts(col(7), col(0), 8.0, OP.is_ge)
+    ts(col(8), col(7), -1.0, OP.mult, 1.0, OP.add)
+    ts(col(9), col(3), -8.0, OP.add)
+    ts(col(10), col(3), 8.0, OP.add)
+    act(v("RST"), v("KEEP", 0, 256), scale=-1048578.0, bias=1048576.0)
+    ts(col(2), col(1), 16.0, OP.mult, 15.0, OP.add)
+    ts(v("SB"), v("YI"), col(2), OP.is_equal)
+    ts(col(11), col(0), 0.0, OP.is_equal)
+    ts(col(12), col(0), 1.0, OP.is_equal)
+    ts(col(13), col(11), 16.0, OP.mult)
+    tt(col(13), col(13), col(12), OP.add)
+    act(v("S16"), v("SB"), scale=32.0)
+    act(v("SN"), v("SB"), scale=col(13))
+    act(v("S0"), v("SB"), scale=col(11))
+    act(v("S256"), v("S0"), scale=256.0)
+    for r in range(16):
+        act(v("SR", 128 * r, 128 * r + 128), v("BO"), scale=v("SELC", r, r + 1))
+    cp(v("SX"), v("C0L"))
+
+    def flip(src, off, lst):
+        for h in (0, 1):
+            if off is None:
+                ts(v("PT", 16 * h, 16 * h + 16), src, col(5 + h), OP.mult)
+            else:
+                ts(v("PT", 16 * h, 16 * h + 16), src, off, OP.add, col(5 + h), OP.mult)
+        run("V", v("PU"), [v("PT")], lambda: g.vector.transpose(out=ap(v("PU")), in_=ap(v("PT"))))
+        tt(lst, v("PU", 0, 16), v("PU", 16, 32), OP.add)
+    flip(v("SX"), None, v("JL"))
+    ts(v("PAM"), YI, col(9), OP.is_equal, col(7), OP.mult)
+    ts(v("PBM"), YI, col(10), OP.is_equal, col(8), OP.mult)
+    ts(v("WI"), v("HWI"), 2047, OP.bitwise_and)
+    cp(v("WF"), v("WI"))
+    for i in (0, 1):
+        ts(v("WU", 8 * i, 8 * i + 8), v("GI", 0, 128, 16), col(1), OP.is_equal, v("WF", i, i + 1), OP.mult)
+    ts(v("KI1"), v("KMI"), 2047, OP.bitwise_and)
+    cp(v("KF"), v("KI1"))
+    ts(v("KD"), v("AI", 0, 16), col(0), OP.is_equal, v("KF"), OP.mult)
+    mm(v("pX", 0, 16), v("BOH"), v("KD"))
+    ts(v("KW"), v("pX", 0, 16), v("WF", 0, 1), OP.mult)
+    ts(v("KW2"), v("KW"), 2047, OP.bitwise_and)
+    for j in range(8):
+        tt(v("WK", 16 * j, 16 * j + 16), v("KW2"), v("BO", 16 * j, 16 * j + 16), OP.mult)
+    ts(v("IDH"), YI, col(3), OP.is_equal)
+    ts(v("TSI"), v("AI"), 0.0, OP.mult)
+    A0 = S
+    cp(v("TW", A0, A0 + L), ind(v("TW", 0, S), v("JL")))
+
+    def sel(b, r):
+        return v(b, 15 - r, 143 - r)
+
+    def srow(r):
+        return v("SR", 128 * r, 128 * r + 128)
+
+    def setup_b():
+        act(v("NW", A0, A0 + L), ind(v("NW", 0, S), v("JL")))
+        act(v("NW", A0 + L, WID), v("KEEP", 0, WID - A0 - L), scale=0.0)
+        act(v("TW", A0 + L, WID), v("KEEP", 0, WID - A0 - L), scale=0.0)
+        prefill()
+        fill(v("U", S, WID), 0.0)
+
+    def prefill():
+        act(v("ASKW", 0, CAP), v("KEEP", 0, CAP), scale=0.0, bias=1024.0)
+        act(v("SLW", 0, CAP), v("S512"))
+        act(v("J0", 0, 256), v("KEEP", 0, 256), scale=0.0)
+
+    def setup_c():
+        cp(v("THF", 0, 1, p=8), v("THI", p=8))
+        ts(v("E8", p=8), v("GI", p=8), v("COL", 3, 4, p=8), OP.is_equal)
+        mm(v("pX", 16, 17), v("E8", p=8), v("THF", 0, 1, p=8))
+        ts(v("TH16"), v("pX", 16, 17), 32.0, OP.mult, -30.0, OP.add)
+        cp(v("THR"), v("TH16"))
+        ts(v("TMPC"), v("AI", 0, 128), col(0), OP.is_gt)
+        tt(v("TRI"), v("TMPC"), v("BO"), OP.mult)
+        ts(col(14), col(0), 16.0, OP.mult)
+        ts(v("DLP"), v("AI", 0, 16), col(14), OP.add, 272.0, OP.add)
+        ts(v("FOUR"), v("DLP"), 272.0 + 254.0, OP.is_equal, 1600.0, OP.mult)
+        ts(v("FOUR"), v("FOUR"), 4.0, OP.add)
+        fill(v("ZERO"), 0.0)
+        fill(v("CE", 0, 1), 0.0)
+        fill(v("SC", 0, 1), 0.0)
+
+    def setup_d():
+        ts(v("MASK"), v("AI"), col(0), OP.is_equal)
+        ts(PA, PIX, 1, OP.add)
+        ts(PG, PA, 15, OP.bitwise_and)
+        ts(col(4), PG, 2.0, OP.mult)
+        ts(v("BO300"), v("BO"), 300.0, OP.mult)
+        ts(v("DC0"), v("CL0"), col(0), OP.add, float(S), OP.add)
+        ts(v("DC1"), v("DC0"), float(AREA), OP.add)
+        ts(v("DC2"), v("DC0"), float(DL - S), OP.add)
+        for i in "012":
+            ts(v("DD" + i), v("DC" + i), 1.0, OP.add)
+        fill(v("C255"), 255.0)
+        fill(v("ONE"), 1.0)
+        fill(v("RESP"), 0.0)
+
+    def hash_a(z, zc, n):
+        m = min(n, 128)
+        nb = (n + 127) // 128
+        for b in range(nb):
+            for i in (0, 1):
+                mm(v("pUV", 16 * i + 8 * b, 16 * i + 8 * b + 8, p=m), v(z, zc + 128 * b, zc + 128 * b + m), v("WU", 8 * i, 8 * i + 8))
+        mm(v("pS", 0, n), v("WK"), v(z, zc, zc + n), True, False)
+        cp(v("UVI", p=m), v("pUV", 0, 32, p=m))
+        ts(v("UVM", p=m), v("UVI", p=m), 2047, OP.bitwise_and)
+        tt(v("TT", p=m), v("UVM", 0, 16, p=m), v("UVM", 16, 32, p=m), OP.mult)
+        k = 8 * nb
+        ts(v("TSI", 0, 16 * k, 16, p=m), v("TT", 0, k, p=m), 5, OP.arith_shift_right, 2047, OP.bitwise_and)
+        scan(v("TXF", 0, 16 * k, p=m), v("KEEP", 0, 16 * k, p=m), v("TSI", 0, 16 * k, p=m), OP.mult, OP.add)
+        for b in range(nb):
+            mm(v("pS", 128 * b, 128 * b + m), v("TXF", 128 * b, 128 * b + 128, p=m), v("IDH", 0, m, p=m), False, b == nb - 1)
+
+    def hash_b(n):
+        cp(v("HI", 0, n), v("pS", 0, n))
+        ts(v("HM", 0, n), v("HI", 0, n), 2047, OP.bitwise_and)
+        cp(v("H16", 0, n), v("HM", 0, n))
+
+    def expand(k0, k1):
+        scan(v("ZX", 16 * k0, 16 * k1), v("KEEP", 0, 16 * (k1 - k0)), v("ZS", 16 * k0, 16 * k1), OP.mult, OP.add)
+
+    def dist(cuts, n, hooks):
+        for i, (k0, k1) in enumerate(cuts):
+            x = v("DF", 16 * k0, 16 * k1)
+            tt(x, ind(v("U", 0, S), v("H16", k0, k1)), v("ZX", 16 * k0, 16 * k1), OP.subtract)
+            act(x, x, AF.Abs)
+            for h in hooks.get(i, ()):
+                h()
+            for r in range(k0 // 16, k1 // 16):
+                mm(v("pD", 0, 256), sel("S16", r), v("DF", 256 * r, 256 * r + 256), r == 0, r == n // 16 - 1)
+        for h in hooks.get("tail", ()):
+            h()
+        scan(v("KY"), v("RST"), v("pD", 0, 256), OP.add, OP.min)
+
+    KEY = v("KY", 15, 256, 16)
+
+    def choose(n, own, dc, lst, hook):
+        k = n // 16
+        ts(v("PQ"), KEY, v("THR"), OP.is_ge)
+        if own:
+            tt(v("XN"), v("PQ"), v("NN"), OP.mult)
+            scan(v("SC", 1, 17), v("XN"), v("ZERO"), OP.add, OP.add)
+            mm(v("pX", 16, 17), v("TRI"), v("SC", 16, 17))
+        ts(v("MC"), KEY, 30, OP.bitwise_and)
+        if own:
+            tt(v("NE"), v("PQ"), v("NZ"), OP.max)
+        tt(v("CODE"), v("NE") if own else v("PQ"), v("MC"), OP.add)
+        for r in range(k):
+            mm(v("pC", 16 * r, 16 * r + 16), srow(r), v("CODE"))
+        hook()
+        ts(v("OH", 0, n), v("pC", 0, n), col(4), OP.is_equal)
+        tt(v("HO", 0, n), v("OH", 0, n), v("HM", 0, n), OP.mult)
+        h1 = v("pC", 256, 256 + n)
+        mm(h1, v("BOH"), v("OH", 0, n), True, False)
+        mm(h1, v("BOH"), v("HO", 0, n), False, True)
+        mm(v("pN", 0, n), v("BO300"), v("OH", 0, n), True, False)
+        tt(v("M1", 0, n), h1, v("MASK", 0, n), OP.mult)
+        cp(v("HR", 0, n), h1)
+        scan(v("LS", 0, n), v("KEEP", 0, n), v("M1", 0, n), OP.mult, OP.add)
+        tt(v("EI", 0, n), h1, v("LS", 0, n), OP.is_equal)
+        mm(v("pN", 0, n), v("BO"), v("EI", 0, n), False, False)
+        kv = 11 if own else k - 1
+        o = [0]
+        for c in range(k - 1):
+            o.append(o[c] + n - 16 * (c + 1))
+        for c in range(kv, k - 1):
+            act(v("EA", o[c] - o[kv], o[c + 1] - o[kv]), v("pC", 256 + 16 * (c + 1), 256 + n), AF.Abs, -1.0, v("LS", 16 * c + 15, 16 * c + 16))
+        if kv < k - 1:
+            act(v("EB", o[kv], o[k - 1]), v("EA", 0, o[k - 1] - o[kv]), AF.Relu, -1.0, 1.0)
+        for c in range(k - 1):
+            if c < kv:
+                ts(v("EB", o[c], o[c + 1]), v("HR", 16 * (c + 1), n), v("LS", 16 * c + 15, 16 * c + 16), OP.is_equal)
+            mm(v("pN", 16 * (c + 1), n), v("BO"), v("EB", o[c], o[c + 1]), False, c == k - 2)
+        HL = v("LS", 15, n, 16)
+        tt(v("HD", 0, k), HL, v("DD" + dc[2], 0, k), OP.subtract)
+        tt(v("CM", 0, n), v("pN", 0, n), v("MASK", 0, n), OP.mult)
+        scan(v("CS", 0, n), v("KEEP", 0, n), v("CM", 0, n), OP.mult, OP.add)
+        ts(v("WA", 0, k), v("CS", 15, n, 16), 301.0, OP.is_equal)
+        tt(v("WM", 0, k), v("WA", 0, k), v("HD", 0, k), OP.mult)
+        tt(v(lst, 0, k), v("WM", 0, k), v(dc, 0, k), OP.add)
+
+    def numbers(A):
+        for r in range(16):
+            mm(v("pM", 272, 288), sel("SN", r), v("NW", A + 16 * r, A + 16 * r + 16), r == 0, r == 15)
+
+    def put_course(t):
+        act(v("CF", 16 * t, 16 * t + 16), v("pM", 272, 288))
+        dma("S", T.yc[:, 256 * t:256 * t + 256], v("CF", 16 * t, 16 * t + 16))
+
+    def widths(t):
+        if t:
+            cp(v("CI"), v("pM", 272, 288))
+        ts(v("CW"), v("CI") if t else v("C0L"), 3, OP.bitwise_and)
+        scan(v("CE", 1, 17), v("CW"), v("FOUR"), OP.add, OP.add)
+        mm(v("pX", 16, 17), v("TRI"), v("CE", 16, 17))
+        ts(v("CFI", 0, 17), v("CE", 0, 17), v("pX", 16, 17), OP.add, 0.2, OP.mult)
+        ts(v("F1", 0, 17), v("CFI", 0, 17), 256.0, OP.min)
+        tt(v("NN"), v("F1", 1, 17), v("F1", 0, 16), OP.subtract)
+        ts(v("NZ"), v("NN"), 0.0, OP.is_equal)
+
+    def slots_a():
+        for r in range(16):
+            mm(v("pM", 16 * r, 16 * r + 16), srow(r), v("F1", 0, 16))
+        act(v("F0R"), v("pM", 0, 256))
+        tt(v("DZ"), v("NZ"), v("DLP"), OP.mult)
+        tt(v("PF"), v("DZ"), v("F1", 0, 16), OP.add)
+        flip(v("PF"), None, v("JL"))
+
+    def slots_b():
+        cp(ind(v("J0"), v("JL")), v("CI1"))
+        scan(v("JM"), v("J0", 0, 256), v("J0", 0, 256), OP.max, OP.max)
+        act(v("JF"), v("J0", 0, 256), AF.Sign)
+
+    def slots_m():
+        for b, x in (("S0", "JM"), ("S256", "JF")):
+            for p in range(16):
+                mm(v("pM", 256, 272), sel(b, p), v(x, p, 256, 16), b == "S0" and p == 0, b == "S256" and p == 15)
+
+    def slots_c():
+        cp(ind(v("SLW"), v("APL")), v("F0R"))
+        tt(v("SLM"), v("SLW", 0, CAP), v("MASK", 0, CAP), OP.mult)
+        scan(v("SLS"), v("KEEP", 0, CAP), v("SLM"), OP.mult, OP.add)
+
+    for t in range(RO):
+        A = S + AREA * (t % 2)
+        B = S + AREA * (1 - t % 2)
+        lender = cores[(rank + 1 + t % (N - 1)) % N]
+        asker = cores[(rank - 1 - t % (N - 1)) % N]
+        mm(v("pZ", 0, 256), v("PAM"), v("TW", A, A + L), True, False)
+        mm(v("pZ", 0, 255), v("PBM"), v("TW", A + 1, A + L), False, True)
+        cp(v("ZB"), v("pZ", 0, 256))
+        for m in range(16):
+            act(v("ZX", 1536 + m, 4096, 16), v("ZB", 96, 256))
+        cp(v("ZS", 0, 1536, 16), v("ZB", 0, 96))
+        hash_a("ZB", 0, 256)
+        if t == 0:
+            setup_b()
+        else:
+            cp(ind(v("NW", A, A + AREA), v("FIX", 0, 3)), v("NB", CAP * (t - 1), CAP * t))
+            numbers(A)
+        expand(0, 64)
+        hash_b(256)
+
+        def course():
+            expand(64, 96)
+            if t == 0:
+                setup_c()
+            widths(t)
+            if t:
+                put_course(t - 1)
+        dist(CUTS, 256, {0: [course], "tail": [setup_d] * (t == 0) + [slots_a]})
+
+        def ask():
+            ts(v("E2"), v("XN"), 0.0, OP.is_equal)
+            tt(v("E2"), v("E2"), v("DLP"), OP.mult)
+            tt(v("SX"), v("SC", 0, 16), v("E2"), OP.add)
+            flip(v("SX"), v("pX", 16, 17), v("APL"))
+            cp(ind(v("ASKW"), v("APL")), v("ZB"))
+            send(lender, v("ASKL", CAP * t, CAP * t + CAP), v("ASKW", 0, CAP), "aa%d" % t, "la%d" % t)
+            arrives(v("ASKL", CAP * t, CAP * t + CAP), asker, "aa%d" % t)
+        choose(256, True, "DC%d" % (t % 2), "LAY", ask)
+        cp(ind(v("U", 0, DL), v("LAY")), v("C255"))
+        if t < RO - 1:
+            act(v("TW", A + L, A + 2 * L), ind(v("TW", 0, A + L), v("LAY")))
+        act(v("NW", A + L, A + 2 * L), ind(v("NW", 0, A + L), v("LAY")))
+        z = CAP * t
+        hash_a("ASKL", z, CAP)
+        cp(v("ZS", 0, 16 * CAP, 16), v("ASKL", z, z + CAP))
+        expand(0, CAP)
+        hash_b(CAP)
+        dist([(0, 32), (32, 48)], CAP, {"tail": [slots_b]})
+        choose(CAP, False, "DC2", "LEN", lambda: None)
+        slots_m()
+        act(v("RESP", 48, 96), ind(v("TW"), v("LEN", 0, 3)))
+        cp(v("RESP", 0, 48), ind(v("U"), v("LEN", 0, 3)))
+        ts(v("RESP", 96, 99), v("LEN", 0, 3), float(DL), OP.is_ge, 256.0, OP.mult)
+        send(asker, v("RETL", RETN * t, RETN * t + RETN), v("RESP"), "ar%d" % t, "lr%d" % t)
+        arrives(v("RETL", RETN * t, RETN * t + RETN), lender, "ar%d" % t)
+        slots_c()
+        ts(v("SLOT"), v("pM", 256, 272), -1.0, OP.add)
+        cp(ind(v("U"), v("LEN", 0, 3)), v("C255", 0, 48))
+        if t < RO - 1:
+            act(v("TW", B, B + L), ind(v("TW", A, A + 2 * L), v("SLOT")))
+        act(v("NW", B, B + L), ind(v("NW", A, A + 2 * L), v("SLOT")))
+        if t < RO - 1:
+            act(v("U", DL, WID), v("KEEP", 0, CAP), scale=0.0)
+            prefill()
+            mm(v("pX", 18, 19), v("ONE"), v("SC", 16, 17))
+            cp(v("PIN"), v("pX", 18, 19))
+            ts(v("PI2"), v("PIN"), 63, OP.bitwise_and)
+            ts(v("THR"), v("PI2"), 32.0, OP.mult, v("TH16"), OP.add)
+        r0 = RETN * t
+        tt(v("FIX", 0, 3), v("SLS", 15, CAP, 16), v("RETL", r0 + 96, r0 + 99), OP.add)
+        if t < RO - 1:
+            cp(ind(v("TW", B, B + AREA), v("FIX", 0, 3)), v("RETL", r0 + 48, r0 + 96))
+        act(v("UB", CAP * t, CAP * t + CAP), v("RETL", r0, r0 + 48))
+    dma("S", T.yu[:, 0:S], v("U", 0, S))
+    B = S + AREA * (RO % 2)
+    cp(ind(v("NW", B, B + AREA), v("FIX", 0, 3)), v("NB", CAP * (RO - 1), CAP * RO))
+    numbers(B)
+    put_course(RO - 1)
+    dma("S", T.yu[:, S:S + RO * CAP], v("UB"))
+    for s in ("sV", "sA", "sP", "sG"):
+        g.wait_ge(T.sem[s], count[s])
+    for i in range(ndma[0]):
+        g.sync.wait_ge(T.sem["d%d" % i], 16)
+    for t in range(RO):
+        lender = cores[(rank + 1 + t % (N - 1)) % N]
+        asker = cores[(rank - 1 - t % (N - 1)) % N]
+        for s, n in (("la", len(engs(core, lender))), ("lr", len(engs(core, asker))), ("aa", len(engs(asker, core))), ("ar", len(engs(lender, core)))):
+            g.wait_ge(T.sem[s + str(t)], n)

@@ -1,43 +1,49 @@
 from concourse.mybir import AluOpType as OP, ActivationFunctionType as AF
 
 RO, CAP, L, S = 5, 48, 256, 2048
+DL = S
+A0 = S + 64
 AREA = 560
-DL = S + 2 * AREA
-WID = DL + CAP
-ASKN = 800
-RETN = 104
+WID = A0 + 2 * AREA
+WIN = 272
+RETN = 56
+BIG = 4096.0
+ROUND = 1.5 * 2.0 ** 34
 
 _sb = {
     "U": (WID, "bfloat16"), "TW": (WID, "bfloat16"), "NW": (WID, "bfloat16"), "NH": (S, "bfloat16"),
     "C0L": (16, "int32"), "HWI": (2, "int32"), "KMI": (1, "int32"), "THI": (1, "int32"),
-    "PIX": (1, "int32"), "PA_": (1, "int32"), "PG_": (1, "int32"), "COL": (16, "float32"), "SELC": (16, "float32"),
+    "PIX": (1, "int32"), "PA_": (1, "int32"), "PG_": (1, "int32"), "PB_": (1, "int32"), "PC_": (1, "int32"), "PD_": (1, "int32"),
+    "COL": (32, "float32"), "SELC": (16, "float32"),
     "GI": (128, "float32"), "YI": (144, "float32"), "AI": (256, "float32"),
-    "BO": (128, "bfloat16"), "BOH": (128, "float16"), "IDH": (128, "float16"), "SB": (144, "bfloat16"), "S16": (144, "bfloat16"), "SN": (144, "bfloat16"),
-    "S0": (144, "bfloat16"), "S256": (144, "bfloat16"), "SR": (2048, "bfloat16"), "PAM": (128, "bfloat16"), "PBM": (128, "bfloat16"),
-    "TRI": (128, "bfloat16"), "SHB": (128, "bfloat16"), "ONE": (128, "bfloat16"), "RST": (256, "float32"), "KEEP": (1024, "bfloat16"), "EA": (336, "float32"),
-    "MASK": (256, "bfloat16"), "DLP": (16, "float32"), "DLP32": (16, "float32"), "CL0": (16, "float32"),
-    "DC0": (16, "float32"), "DC1": (16, "float32"), "DC2": (16, "float32"), "DD0": (16, "float32"), "DD1": (16, "float32"),
-    "DD2": (16, "float32"), "FIXC": (16, "float32"), "FOUR": (16, "float32"),
-    "ZERO": (16, "float32"), "CI1": (256, "bfloat16"), "NB": (240, "bfloat16"), "C255": (256, "bfloat16"),
-    "S512": (48, "float32"), "E8": (128, "float32"), "THF": (16, "float32"), "TH16": (1, "float32"), "THR": (1, "float32"),
-    "WU": (16, "float16"), "WK": (128, "float16"), "WF": (2, "float32"), "WI": (2, "int32"), "KD": (16, "float16"), "KF": (1, "float32"),
-    "KI1": (1, "int32"), "KW": (16, "int32"), "KW2": (16, "int32"), "TMPC": (128, "float32"),
+    "BO": (128, "bfloat16"), "BO4": (128, "bfloat16"), "BON": (128, "bfloat16"), "IDB": (128, "bfloat16"), "SB": (144, "bfloat16"),
+    "S16": (144, "bfloat16"), "SN": (144, "bfloat16"), "S0": (144, "bfloat16"), "S0N": (144, "bfloat16"), "S15": (144, "bfloat16"),
+    "SR": (2048, "bfloat16"), "PAM": (128, "bfloat16"), "PBM": (128, "bfloat16"), "HID": (128, "bfloat16"), "DM": (128, "bfloat16"),
+    "SHM": (128, "bfloat16"), "TRI": (128, "bfloat16"), "ONE": (256, "bfloat16"), "NEG": (128, "bfloat16"), "E0": (128, "bfloat16"),
+    "HALF": (128, "float16"), "M2": (256, "bfloat16"), "MB": (256, "bfloat16"), "R0": (256, "float32"), "RST": (256, "float32"),
+    "KEEP": (1024, "bfloat16"), "CL0": (16, "float32"), "DC0": (16, "float32"), "DC1": (16, "float32"), "DC2": (16, "float32"),
+    "FOUR": (16, "float32"), "IB": (16, "float32"), "SI": (16, "bfloat16"), "KC": (16, "float32"),
+    "NB": (240, "bfloat16"), "C255": (256, "bfloat16"), "E8": (128, "float32"), "THF": (16, "float32"), "TH32": (1, "float32"),
+    "THR": (1, "float32"), "WA": (144, "float16"), "WL": (144, "float16"), "WR": (144, "float16"), "WF": (2, "float32"), "WI": (2, "int32"),
+    "KD": (16, "float16"), "KF": (1, "float32"), "KI1": (1, "int32"), "KW": (16, "int32"), "KW2": (16, "int32"), "TMPC": (128, "float32"),
+    "PT": (32, "float32"), "PU": (32, "float32"), "JL": (16, "uint16"),
     "ZB": (256, "bfloat16"), "UVI": (32, "int32"), "UVM": (32, "int32"), "TT": (16, "int32"), "TSI": (256, "int32"),
-    "BO300": (128, "float16"), "TXF": (256, "float16"), "HI": (256, "int32"), "HM": (256, "int32"), "H16": (256, "uint16"),
-    "ZS": (1536, "bfloat16"), "ZX": (4096, "bfloat16"), "DF": (4096, "bfloat16"), "KY": (256, "int32"),
-    "PQ": (16, "float32"), "XN": (16, "bfloat16"), "SC": (32, "bfloat16"), "SX": (16, "float32"), "E2": (16, "float32"), "PT": (32, "float32"),
-    "PU": (32, "float32"), "APL": (16, "uint16"), "ASKW": (ASKN, "bfloat16"), "PIN": (1, "int32"), "PI2": (1, "int32"),
-    "MC": (16, "int32"), "P32": (16, "float32"), "NE": (16, "float32"), "CODE": (16, "bfloat16"), "OH": (256, "float16"), "HO": (256, "float16"),
-    "HR": (256, "float16"), "M1": (256, "float32"), "LS": (256, "float32"), "EI": (256, "bfloat16"), "EB": (1920, "bfloat16"),
-    "EL": (16, "float32"), "HD": (16, "float32"), "HMM": (16, "float32"), "CM": (256, "float32"), "CS": (256, "float32"), "WA": (16, "float32"),
-    "WM": (16, "float32"), "LAY": (16, "uint16"), "LEN": (4, "uint16"),
+    "TXF": (256, "float16"), "Y": (256, "float32"), "H16": (256, "uint16"), "HM": (256, "float16"),
+    "HL": (WIN, "int32"), "H16L": (48, "uint16"), "HML": (48, "float16"),
+    "ZS": (1024, "bfloat16"), "ZX": (4096, "bfloat16"), "DF": (4096, "bfloat16"), "KY": (256, "int32"),
+    "ZSL": (768, "bfloat16"), "ZXL": (768, "bfloat16"), "DFL": (768, "bfloat16"),
+    "PQ": (16, "bfloat16"), "XN": (16, "bfloat16"), "CUM": (WIN, "bfloat16"), "CNT": (4, "float32"), "LST": (4, "uint16"),
+    "JUNK": (256, "bfloat16"), "GA": (48, "bfloat16"), "GB": (48, "bfloat16"), "PIN": (1, "int32"), "PI2": (1, "int32"),
+    "MC": (16, "int32"), "CODE": (16, "bfloat16"), "OH": (256, "float16"), "HO": (256, "float16"),
+    "HR": (256, "float16"), "LS": (256, "float32"), "EI": (256, "bfloat16"), "EB": (1920, "bfloat16"), "EA": (336, "float32"),
+    "CS": (256, "float32"), "LAY": (16, "uint16"), "LEN": (4, "uint16"),
     "CI": (16, "int32"), "CW": (16, "int32"), "CE": (32, "bfloat16"), "CFI": (32, "int32"), "F1": (32, "bfloat16"),
-    "NN": (16, "bfloat16"), "NZ": (16, "float32"), "DZ": (16, "float32"), "PF": (16, "float32"), "JL": (16, "uint16"),
-    "J0": (ASKN, "bfloat16"), "JM": (256, "bfloat16"), "JF": (256, "bfloat16"), "SLOT": (16, "uint16"),
-    "F0R": (256, "float32"), "SLW": (ASKN, "float32"), "SLM": (48, "float32"), "SLS": (48, "float32"), "FIX": (4, "uint16"), "CF": (80, "float32"),
-    "ASKL": (RO * CAP, "bfloat16"), "RESP": (RETN, "bfloat16"), "RETL": (RO * RETN, "bfloat16"), "UB": (240, "bfloat16"),
+    "NN": (16, "bfloat16"), "NZ": (16, "float32"), "F0R": (WIN, "bfloat16"), "JC": (16, "float32"), "JN": (32, "float16"),
+    "JF": (16, "float32"), "SLOT": (16, "uint16"), "FIX": (4, "uint16"), "CF": (80, "float32"),
+    "ZL": (RO * WIN, "bfloat16"), "LSL": (RO * 8, "uint16"), "RESP": (RETN, "bfloat16"), "RESU": (CAP, "bfloat16"),
+    "RETL": (RO * RETN, "bfloat16"), "UB": (240, "bfloat16"),
 }
-_ps = ("pZ", "pUV", "pS", "pD", "pC", "pN", "pX", "pM")
+_ps = ("pA", "pB", "pS", "pD", "pC", "pH", "pN", "pX")
 _place = {}
 _fill = {}
 for _k in _sb:
@@ -49,8 +55,13 @@ SCRATCH = {k: ("sbuf", [128, _sb[k][0]], _sb[k][1]) for k in _sb if k not in _pl
 SCRATCH.update({"pack_" + k: ("sbuf", [128, _fill[k]], k) for k in _fill})
 SCRATCH.update({k: ("psum", [128, 512], "float32") for k in _ps})
 _bytes = {"bfloat16": 2, "float16": 2, "uint16": 2, "float32": 4, "int32": 4}
-SEMAPHORES = ["sV", "sA", "sP", "sG"] + ["d%d" % i for i in range(16)] + [a + str(t) for a in ("la", "lr", "aa", "ar") for t in range(RO)]
-CUTS = [(0, 64), (64, 96), (96, 160), (160, 208), (208, 240), (240, 256)]
+MSG = ("z", "q", "a", "u")
+SEMAPHORES = ["sV", "sA", "sP", "sG"] + ["d%d" % i for i in range(16)] + [e + m + str(t) for e in "lr" for m in MSG for t in range(RO)]
+CUTS = [0, 32, 64, 96, 128, 160, 192, 224, 240, 256]
+VX = 64
+AX = [64, 160, 256]
+KV = 12
+LEAST, WAKE, GATHER, SCATTER, FAR, NEAR = 64, 140, 1.5, 3.5, 2600, 1600
 
 
 def rank_program(g, core, T, topo):
@@ -60,11 +71,6 @@ def rank_program(g, core, T, topo):
     cores = list(T.cores)
     N = len(cores)
     Q = {"V": g.vector, "A": g.scalar, "P": g.tensor, "G": g, "S": g.sync}
-    count = {"sV": 0, "sA": 0, "sP": 0, "sG": 0}
-    know = {q: {} for q in Q}
-    snap = {}
-    hist = {}
-    ndma = [0]
 
     def v(b, c0=0, c1=None, st=1, p=128, rows=None):
         p = rows or p
@@ -77,6 +83,8 @@ def rank_program(g, core, T, topo):
         return ("I", w, o)
 
     def ap(x):
+        if not isinstance(x, tuple):
+            return x
         if x[0] == "I":
             return ap(x[1]).indirect(ap(x[2]))
         b, c0, c1, st, p = x
@@ -87,474 +95,539 @@ def rank_program(g, core, T, topo):
             return t[:, c0:c1] if p == 128 else t[0:p, c0:c1]
         return t[:, c0:c1:st] if p == 128 else t[0:p, c0:c1:st]
 
-    def span(x):
-        n = _bytes[SCRATCH[x[0]][2]]
-        return x[0], x[1] * n // 16, (x[2] * n + 15) // 16
+    def size(x):
+        return 16 * size(x[2]) if x[0] == "I" else len(range(x[1], x[2], x[3]))
 
-    def learn(q, sem, val):
-        k = know[q]
-        if k.get(sem, 0) >= val:
-            return
-        k[sem] = val
-        for s2, v2 in snap.get((sem, val), {}).items():
-            if k.get(s2, 0) < v2:
-                k[s2] = v2
+    def width(x):
+        return _bytes[SCRATCH[x[1][0] if x[0] == "I" else x[0]][2]]
 
-    def need(q, rd, wr):
-        deps = {}
-        for x, w in [(x, False) for x in rd] + [(x, True) for x in wr]:
-            b, lo, hi = span(x)
-            ps = SCRATCH[b][0] == "psum"
-            keep = []
-            for e in hist.get(b, []):
-                elo, ehi, ew, eq, es, ev = e
-                hit = (ps and eq != q) or (not ps and elo < hi and lo < ehi)
-                if hit and (w or ew or ps):
-                    if deps.get(es, 0) < ev:
-                        deps[es] = ev
-                    if ps or (w and lo <= elo and ehi <= hi):
-                        continue
-                keep.append(e)
-            hist[b] = keep
-        for s in sorted(deps):
-            if know[q].get(s, 0) < deps[s]:
-                Q[q].wait_ge(T.sem[s], deps[s])
-                learn(q, s, deps[s])
+    def psum(b):
+        return SCRATCH[b][0] == "psum"
 
-    def note(q, rd, wr, sem, val):
-        snap[(sem, val)] = dict(know[q])
-        for x, w in [(x, False) for x in rd] + [(x, True) for x in wr]:
-            b, lo, hi = span(x)
-            h = hist.setdefault(b, [])
-            h[:] = [e for e in h if not (e[0] == lo and e[1] == hi and e[2] == w and e[3] == q and e[4] == sem)]
-            h.append((lo, hi, w, q, sem, val))
+    def cols(x, blocks):
+        b, c0, c1, st, p = x
+        if blocks:
+            n = 16 // width(x)
+            c0, c1, st = c0 // n * n, (c1 + n - 1) // n * n, 1
+        if st == 1:
+            return ((1 << (c1 - c0)) - 1) << c0
+        return sum(1 << c for c in range(c0, c1, st))
 
-    def a_(x):
-        return ap(x) if isinstance(x, tuple) else x
+    ops = []
+    reads, writes, last_pe = {}, {}, {}
 
-    def run(q, out, ins, f):
+    def add(q, out, ins, f, dur, lat=0, own=None, after=()):
         rd, wr = [], []
         for x in ins:
             if isinstance(x, tuple):
                 rd += [x[1], x[2]] if x[0] == "I" else [x]
+        if isinstance(out, tuple):
+            if out[0] == "I":
+                wr.append(out[1])
+                rd.append(out[2])
+            else:
+                wr.append(out)
+        i = len(ops)
+        pre = set()
+        for x in rd:
+            m = cols(x, own is not None)
+            pre.update(j for mj, j in writes.get(x[0], []) if m & mj)
+        for x in wr:
+            b, m = x[0], cols(x, own is not None)
+            pre.update(j for mj, j in writes.get(b, []) + reads.get(b, []) if m & mj)
+            if q == "P":
+                pre.update(last_pe.get(b, []))
+                last_pe[b] = [i]
+            if x[4] == 128 and out[0] != "I":
+                writes[b] = [e for e in writes.get(b, []) if e[0] & ~m]
+                reads[b] = [e for e in reads.get(b, []) if e[0] & ~m]
+            elif out[0] == "I":
+                writes[b] = [e for e in writes.get(b, []) if e[0] & ~m]
+                reads[b] = [e for e in reads.get(b, []) if e[0] & ~m]
+            writes.setdefault(b, []).append((m, i))
+        for x in rd:
+            reads.setdefault(x[0], []).append((cols(x, own is not None), i))
+        ops.append({"q": q, "f": f, "dur": dur, "lat": lat, "pre": pre, "after": set(after), "own": own,
+                    "banks": {x[0] for x in rd + wr if psum(x[0])}})
+        return i
+
+    def vlen(out, ins, two=False):
+        full = [x for x in [out] + ins if isinstance(x, tuple) and size(x) == size(out)]
         if out[0] == "I":
-            wr.append(out[1])
-            rd.append(out[2])
-        else:
-            wr.append(out)
-        need(q, rd, wr)
-        s = "s" + q
-        count[s] += 1
-        f().then_inc(T.sem[s], 1)
-        note(q, rd, wr, s, count[s])
+            return 50 + SCATTER * size(out)
+        if any(x[0] == "I" for x in full):
+            return 50 + GATHER * size(out)
+        r = 0.5 if all(width(x) == 2 for x in full) else 1.0
+        return max(LEAST, size(out) * r * (2 if two and not any(psum(x[0]) for x in ins) else 1))
 
     def cp(out, in_):
-        run("V", out, [in_], lambda: g.vector.tensor_copy(out=ap(out), in_=ap(in_)))
+        add("V", out, [in_], lambda: g.vector.tensor_copy(out=ap(out), in_=ap(in_)), vlen(out, [in_]))
 
     def tt(out, a, b, op):
-        run("V", out, [a, b], lambda: g.vector.tensor_tensor(out=ap(out), in0=ap(a), in1=ap(b), op=op))
+        add("V", out, [a, b], lambda: g.vector.tensor_tensor(out=ap(out), in0=ap(a), in1=ap(b), op=op), vlen(out, [a, b], True))
 
     def ts(out, a, s1, op0, s2=None, op1=None):
         if op1 is None:
-            run("V", out, [a, s1], lambda: g.vector.tensor_scalar(out=ap(out), in0=ap(a), scalar1=a_(s1), scalar2=None, op0=op0))
+            add("V", out, [a, s1], lambda: g.vector.tensor_scalar(out=ap(out), in0=ap(a), scalar1=ap(s1), scalar2=None, op0=op0), vlen(out, [a]))
         else:
-            run("V", out, [a, s1, s2], lambda: g.vector.tensor_scalar(out=ap(out), in0=ap(a), scalar1=a_(s1), scalar2=a_(s2), op0=op0, op1=op1))
+            add("V", out, [a, s1, s2], lambda: g.vector.tensor_scalar(out=ap(out), in0=ap(a), scalar1=ap(s1), scalar2=ap(s2), op0=op0, op1=op1),
+                vlen(out, [a]))
 
-    def scan(out, d0, d1, op0, op1):
-        run("V", out, [d0, d1], lambda: g.vector.tensor_tensor_scan(out=ap(out), data0=ap(d0), data1=ap(d1), initial=0.0, op0=op0, op1=op1))
+    def scan(out, d0, d1, op0, op1, initial=0.0):
+        add("V", out, [d0, d1], lambda: g.vector.tensor_tensor_scan(out=ap(out), data0=ap(d0), data1=ap(d1), initial=initial, op0=op0, op1=op1),
+            vlen(out, [d0, d1]))
 
     def fill(out, c):
-        run("V", out, [], lambda: g.vector.memset(ap(out), c))
+        add("V", out, [], lambda: g.vector.memset(ap(out), c), vlen(out, []))
 
-    def act(out, in_, func=AF.Copy, scale=1.0, bias=0.0):
-        run("A", out, [in_, scale, bias], lambda: g.scalar.activation(out=ap(out), in_=ap(in_), func=func, bias=a_(bias), scale=a_(scale)))
+    def act(out, in_, func=AF.Copy, scale=1.0, bias=0.0, total=None):
+        n = size(out)
+        if total is None:
+            add("A", out, [in_, scale, bias], lambda: g.scalar.activation(out=ap(out), in_=ap(in_), func=func, bias=ap(bias), scale=ap(scale)),
+                65 + GATHER * n if in_[0] == "I" else max(LEAST, n))
+        else:
+            add("A", total, [in_, scale, bias], lambda: g.scalar.activation(out=ap(out), in_=ap(in_), func=func, bias=ap(bias), scale=ap(scale),
+                                                                            accum_out=ap(total)), max(LEAST, n) + 20, after=dumps[-1:])
+            ops[-1]["pre"].update(dumps[-1:])
+            dumps.append(len(ops) - 1)
+    dumps = []
 
     def mm(out, lhsT, rhs, start=True, stop=True):
-        run("P", out, [lhsT, rhs], lambda: g.tensor.matmul(ap(out), ap(lhsT), ap(rhs), start=start, stop=stop))
+        add("P", out, [lhsT, rhs], lambda: g.tensor.matmul(ap(out), ap(lhsT), ap(rhs), start=start, stop=stop),
+            max(min(64, size(lhsT)), size(rhs)) * (2 if width(rhs) == 4 else 0.5))
 
     def iota(out, pat, base=0, cm=0):
         if SCRATCH[out[0]][2] != "int32":
-            run("G", out, [], lambda: g.iota(ap(out), pat, base, cm, allow_small_or_imprecise_dtypes=True))
+            add("G", out, [], lambda: g.iota(ap(out), pat, base, cm, allow_small_or_imprecise_dtypes=True), 130 + 2 * size(out))
         else:
-            run("G", out, [], lambda: g.iota(ap(out), pat, base, cm))
+            add("G", out, [], lambda: g.iota(ap(out), pat, base, cm), 130 + 2 * size(out))
 
-    def dma(q, out, in_):
-        rd = [in_] if isinstance(in_, tuple) else []
-        wr = [out] if isinstance(out, tuple) else []
-        need(q, rd, wr)
-        s = "d%d" % ndma[0]
-        ndma[0] += 1
-        Q[q].dma_start(out=a_(out), in_=a_(in_)).then_inc(T.sem[s], 16)
-        snap[(s, 16)] = dict(know[q])
-        for x, w in [(x, False) for x in rd] + [(x, True) for x in wr]:
-            b, lo, hi = span(x)
-            hist.setdefault(b, []).append((lo, hi, w, "dma", s, 16))
+    dmas = []
+
+    def dma(q, out, in_, lat=NEAR, after=()):
+        s = "d%d" % len(dmas)
+        dmas.append(s)
+        return add(q, out, [in_], lambda: Q[q].dma_start(out=ap(out), in_=ap(in_)).then_inc(T.sem[s], 16), 50, lat, (s, 16), after)
 
     def engs(src, dst):
         return topo.engines(src, dst)[:8]
 
-    def send(dst, out, in_, rsem, lsem):
-        need("G", [in_], [])
-        mask = 0
-        for e in engs(core, dst):
-            mask |= 1 << e
-        rid, pid = topo.addr(dst, core)
-        g.remote_dma(ap(out), ap(in_), T.sem[rsem], T.sem[lsem], pid, rid, mask)
-        b, lo, hi = span(in_)
-        hist.setdefault(b, []).append((lo, hi, False, "rdma", lsem, len(engs(core, dst))))
-        snap[(lsem, len(engs(core, dst)))] = dict(know["G"])
+    far = []
 
-    def arrives(x, src, rsem):
-        b, lo, hi = span(x)
-        hist.setdefault(b, []).append((lo, hi, True, "rdma", rsem, len(engs(src, core))))
+    def message(m, t, dst, src, out, in_):
+        mask = sum(1 << e for e in engs(core, dst))
+        rid, pid = topo.addr(dst, core)
+        ls, rs = ("l%s%d" % (m, t), len(engs(core, dst))), ("r%s%d" % (m, t), len(engs(src, core)))
+        far.extend([ls, rs])
+        i = add("G", None, [in_], lambda: g.remote_dma(ap(out), ap(in_), T.sem[rs[0]], T.sem[ls[0]], pid, rid, mask), 300, FAR, ls)
+        add("N", out, [], None, 0, 0, rs, [i])
 
     dma("S", v("C0L"), T.c0[:])
-    dma("S", v("TW", 0, S), T.tp[:])
+    d_tp = dma("S", v("TW", 0, S), T.tp[:], 2 * NEAR)
     dma("A", v("HWI"), T.hw[:])
     dma("A", v("KMI"), T.km[:])
     dma("A", v("THI", p=8), T.th[:])
-    dma("A", v("U", 0, S), T.us[:])
+    dma("S", v("U", 0, S), T.us[:], 3 * NEAR)
     iota(v("PIX"), [[0, 1]], 0, 1)
     iota(v("GI"), [[1, 8], [0, 16]])
     iota(v("AI"), [[0, 16], [1, 16]])
     iota(v("YI"), [[1, 144]])
     iota(v("CL0"), [[16, 16]])
-    iota(v("NW", 0, S), [[0, 128], [1, 16]])
-    iota(v("NH"), [[1, 128], [0, 16]])
+    iota(v("KC", 0, 12), [[31, 12]], 18)
+    iota(v("KC", 12, 16), [[11, 4]], 386)
+    for h in (0, 1):
+        iota(v("NW", 1024 * h, 1024 * h + 1024), [[0, 64], [1, 16]])
+        iota(v("NH", 1024 * h, 1024 * h + 1024), [[1, 64], [0, 16]], 64 * h)
     dma("S", v("NW", 0, S, rows=(0, 128, 16)), v("NH", 0, S, rows=(0, 8, 1)))
-    iota(v("CI1"), [[1, 256]], 1)
-    iota(v("S512"), [[1, 48]], 256)
     iota(v("NB"), [[0, 15], [1, 16]])
     iota(v("NH", 0, 240), [[1, 15], [0, 16]], 128)
     dma("S", v("NB", rows=(0, 128, 16)), v("NH", 0, 240, rows=(0, 8, 1)))
-    PIX, PA, PG = v("PIX"), v("PA_"), v("PG_")
+    PIX, GI, YI, AI16 = v("PIX"), v("GI"), v("YI", 0, 128), v("AI", 0, 16)
 
     def col(i):
         return v("COL", i, i + 1)
-    ts(PA, PIX, 15, OP.bitwise_and)
-    ts(PG, PIX, 4, OP.arith_shift_right)
-    cp(col(0), PA)
-    cp(col(1), PG)
+    ts(v("PA_"), PIX, 15, OP.bitwise_and)
+    ts(v("PG_"), PIX, 4, OP.arith_shift_right)
+    ts(v("PB_"), PIX, 4, OP.arith_shift_right, 1, OP.bitwise_and)
+    cp(col(0), v("PA_"))
+    cp(col(1), v("PG_"))
     cp(col(3), PIX)
-    GI, YI = v("GI"), v("YI", 0, 128)
+    cp(col(6), v("PB_"))
+    ts(col(5), v("PB_"), -1.0, OP.mult, 1.0, OP.add)
+    ts(col(2), v("PG_"), 16.0, OP.mult, 15.0, OP.add)
+    ts(col(4), v("PA_"), 2.0, OP.mult)
+    ts(col(7), v("PA_"), 8.0, OP.is_ge)
+    ts(col(8), v("PA_"), 8.0, OP.is_lt)
+    ts(col(9), PIX, -8.0, OP.add)
+    ts(col(10), PIX, 8.0, OP.add)
+    ts(col(11), v("PA_"), 0.0, OP.is_equal)
+    ts(col(12), v("PA_"), 0.0, OP.is_equal, -1.0, OP.mult)
+    ts(col(14), v("PA_"), 16.0, OP.mult)
+    ts(col(15), v("PA_"), 15.0, OP.is_equal, -0.5, OP.mult)
+    ts(col(16), v("PA_"), 15.0, OP.is_lt, -0.5, OP.mult)
+    ts(col(17), PIX, 1.0, OP.add)
+    ts(col(18), v("PA_"), 2.0, OP.is_lt)
+    ts(col(13), col(11), 15.0, OP.mult, col(18), OP.add)
     ts(v("BO"), GI, col(1), OP.is_equal)
-    ts(v("SELC"), v("AI", 0, 16), col(0), OP.is_equal)
+    ts(v("SELC"), AI16, col(0), OP.is_equal)
+    ts(v("SB"), v("YI"), col(2), OP.is_equal)
+    ts(v("IDB"), YI, col(3), OP.is_equal)
+    ts(v("PAM"), YI, col(9), OP.is_equal, col(7), OP.mult)
+    ts(v("PBM"), YI, col(10), OP.is_equal, col(8), OP.mult)
     for j in range(4):
         act(v("KEEP", 256 * j, 256 * j + 256), v("AI"), AF.Sign)
-    act(v("ZS", 0, 1024), v("KEEP"), scale=0.0)
-    act(v("ZS", 1024, 1536), v("KEEP", 0, 512), scale=0.0)
-    ts(PA, PIX, 4, OP.arith_shift_right)
-    ts(PG, PA, 1, OP.bitwise_and)
-    cp(col(6), PG)
-    ts(col(5), col(6), -1.0, OP.mult, 1.0, OP.add)
-    cp(v("BOH"), v("BO"))
-    ts(col(7), col(0), 8.0, OP.is_ge)
-    ts(col(8), col(7), -1.0, OP.mult, 1.0, OP.add)
-    ts(col(9), col(3), -8.0, OP.add)
-    ts(col(10), col(3), 8.0, OP.add)
-    act(v("RST"), v("KEEP", 0, 256), scale=-1048578.0, bias=1048576.0)
-    ts(col(2), col(1), 16.0, OP.mult, 15.0, OP.add)
-    ts(v("SB"), v("YI"), col(2), OP.is_equal)
-    ts(col(11), col(0), 0.0, OP.is_equal)
-    ts(col(12), col(0), 1.0, OP.is_equal)
-    ts(col(13), col(11), 16.0, OP.mult)
-    tt(col(13), col(13), col(12), OP.add)
+    K256 = v("KEEP", 0, 256)
+
+    def const(out, c):
+        for j in range(out[1], out[2], 256):
+            n = min(256, out[2] - j)
+            act((out[0], j, j + n, 1, 128), v("AI", 0, n), scale=0.0, bias=c)
+    const(v("ONE"), 1.0)
+    const(v("NEG"), -1.0)
+    const(v("ZS"), 0.0)
+    const(v("ZSL"), 0.0)
+    const(v("R0"), -1048576.0)
+    const(v("C255"), 255.0)
+    const(v("CUM", 0, 1), 0.0)
+    const(v("CUM", 257, WIN), 0.0)
+    const(v("F0R", 256, WIN), 256.0)
+    const(v("CE", 0, 1), 0.0)
+    const(v("CNT", 3, 4), 0.0)
+    const(v("RESP", 48, RETN), 0.0)
+    for b in ("U", "TW", "NW"):
+        const(v(b, S, A0), 0.0)
+        const(v(b, A0 + (0 if b == "U" else L), WID), 0.0)
+    for t in range(RO):
+        const(v("ZL", WIN * t + 256, WIN * t + WIN), 1024.0)
+    act(v("RST"), K256, scale=-1048576.0, bias=1048576.0)
+    act(v("M2"), v("AI"), scale=2.0)
     act(v("S16"), v("SB"), scale=32.0)
     act(v("SN"), v("SB"), scale=col(13))
     act(v("S0"), v("SB"), scale=col(11))
-    act(v("S256"), v("S0"), scale=256.0)
+    act(v("S0N"), v("SB"), scale=col(12))
+    act(v("S15"), v("SB"), scale=col(15))
+    act(v("HID"), v("IDB"), scale=0.5)
+    act(v("BO4"), v("BO"), scale=BIG)
+    act(v("BON"), v("BO"), scale=-BIG)
+    act(v("E0"), v("ONE", 0, 128), scale=col(11))
     for r in range(16):
         act(v("SR", 128 * r, 128 * r + 128), v("BO"), scale=v("SELC", r, r + 1))
-    cp(v("SX"), v("C0L"))
-
-    def flip(src, off, lst):
-        for h in (0, 1):
-            if off is None:
-                ts(v("PT", 16 * h, 16 * h + 16), src, col(5 + h), OP.mult)
-            else:
-                ts(v("PT", 16 * h, 16 * h + 16), src, off, OP.add, col(5 + h), OP.mult)
-        run("V", v("PU"), [v("PT")], lambda: g.vector.transpose(out=ap(v("PU")), in_=ap(v("PT"))))
-        tt(lst, v("PU", 0, 16), v("PU", 16, 32), OP.add)
-    flip(v("SX"), None, v("JL"))
-    ts(v("PAM"), YI, col(9), OP.is_equal, col(7), OP.mult)
-    ts(v("PBM"), YI, col(10), OP.is_equal, col(8), OP.mult)
+    fill(v("HL", 256, WIN), 0)
+    fill(v("TSI"), 0)
+    ts(v("HALF", p=32), v("GI", p=32), 0.0, OP.mult, -1023.5, OP.add)
+    ts(v("JN", 0, 1), PIX, 0.0, OP.mult, -2.0, OP.add)
+    for h in (0, 1):
+        ts(v("PT", 16 * h, 16 * h + 16), v("C0L"), col(5 + h), OP.mult)
+    add("V", v("PU"), [v("PT")], lambda: g.vector.transpose(out=ap(v("PU")), in_=ap(v("PT"))), LEAST)
+    tt(v("JL"), v("PU", 0, 16), v("PU", 16, 32), OP.add)
+    cp(v("TW", A0, A0 + L), ind(v("TW", 0, S), v("JL")))
+    act(v("NW", A0, A0 + L), ind(v("NW", 0, S), v("JL")))
     ts(v("WI"), v("HWI"), 2047, OP.bitwise_and)
     cp(v("WF"), v("WI"))
     for i in (0, 1):
-        ts(v("WU", 8 * i, 8 * i + 8), v("GI", 0, 128, 16), col(1), OP.is_equal, v("WF", i, i + 1), OP.mult)
+        ts(v("WA", 8 * i, 8 * i + 8), v("GI", 0, 128, 16), col(1), OP.is_equal, v("WF", i, i + 1), OP.mult)
     ts(v("KI1"), v("KMI"), 2047, OP.bitwise_and)
     cp(v("KF"), v("KI1"))
-    ts(v("KD"), v("AI", 0, 16), col(0), OP.is_equal, v("KF"), OP.mult)
-    mm(v("pX", 0, 16), v("BOH"), v("KD"))
+    ts(v("KD"), AI16, col(0), OP.is_equal, v("KF"), OP.mult)
+    mm(v("pX", 0, 16), v("BO"), v("KD"))
     ts(v("KW"), v("pX", 0, 16), v("WF", 0, 1), OP.mult)
     ts(v("KW2"), v("KW"), 2047, OP.bitwise_and)
     for j in range(8):
-        tt(v("WK", 16 * j, 16 * j + 16), v("KW2"), v("BO", 16 * j, 16 * j + 16), OP.mult)
-    ts(v("IDH"), YI, col(3), OP.is_equal)
-    ts(v("TSI"), v("AI"), 0.0, OP.mult)
-    A0 = S
-    cp(v("TW", A0, A0 + L), ind(v("TW", 0, S), v("JL")))
+        tt(v("WA", 16 + 16 * j, 32 + 16 * j), v("KW2"), v("BO", 16 * j, 16 * j + 16), OP.mult)
+    mm(v("pN", 0, 144), v("PBM"), v("WA"))
+    mm(v("pC", 0, 144), v("PAM"), v("WA"))
+    cp(v("WL"), v("pN", 0, 144))
+    cp(v("WR"), v("pC", 0, 144))
+    cp(v("THF", 0, 1, p=8), v("THI", p=8))
+    ts(v("E8", p=8), v("GI", p=8), v("COL", 3, 4, p=8), OP.is_equal)
+    mm(v("pX", 16, 17), v("E8", p=8), v("THF", 0, 1, p=8))
+    ts(v("TH32"), v("pX", 16, 17), 32.0, OP.mult, -1.0, OP.add)
+    cp(v("THR"), v("TH32"))
+    ts(v("TMPC"), v("AI", 0, 128), col(0), OP.is_gt)
+    tt(v("TRI"), v("TMPC"), v("BO"), OP.mult)
+    ts(v("SHM"), YI, col(17), OP.is_equal, col(16), OP.mult)
+    tt(v("DM"), v("SHM"), v("HID"), OP.add)
+    ts(v("MB"), v("AI"), col(0), OP.not_equal, 2 * BIG, OP.mult)
+    ts(v("FOUR"), AI16, col(14), OP.add, 254.0, OP.is_equal)
+    ts(v("FOUR"), v("FOUR"), 1600.0, OP.mult, 4.0, OP.add)
+    ts(v("SI"), v("CL0"), col(0), OP.add)
+    ts(v("IB"), v("CL0"), col(0), OP.add, 0.5, OP.add)
+    ts(v("DC0"), v("CL0"), col(0), OP.add, float(A0), OP.add)
+    ts(v("DC1"), v("CL0"), col(0), OP.add, float(A0 + AREA), OP.add)
+    ts(v("DC2"), v("CL0"), col(0), OP.add, float(DL), OP.add)
 
     def sel(b, r):
         return v(b, 15 - r, 143 - r)
 
-    def srow(r):
-        return v("SR", 128 * r, 128 * r + 128)
+    def spread(out, c0, x, k=16):
+        for r in range(k):
+            mm(v(out, c0 + 16 * r, c0 + 16 * r + 16), v("SR", 128 * r, 128 * r + 128), x)
 
-    def setup_b():
-        act(v("NW", A0, A0 + L), ind(v("NW", 0, S), v("JL")))
-        act(v("NW", A0 + L, WID), v("KEEP", 0, WID - A0 - L), scale=0.0)
-        act(v("TW", A0 + L, WID), v("KEEP", 0, WID - A0 - L), scale=0.0)
-        prefill()
-        fill(v("U", S, WID), 0.0)
-
-    def prefill():
-        act(v("ASKW", 0, CAP), v("KEEP", 0, CAP), scale=0.0, bias=1024.0)
-        act(v("SLW", 0, CAP), v("S512"))
-        act(v("J0", 0, 256), v("KEEP", 0, 256), scale=0.0)
-
-    def setup_c():
-        cp(v("THF", 0, 1, p=8), v("THI", p=8))
-        ts(v("E8", p=8), v("GI", p=8), v("COL", 3, 4, p=8), OP.is_equal)
-        mm(v("pX", 16, 17), v("E8", p=8), v("THF", 0, 1, p=8))
-        ts(v("TH16"), v("pX", 16, 17), 32.0, OP.mult, -30.0, OP.add)
-        cp(v("THR"), v("TH16"))
-        ts(v("TMPC"), v("AI", 0, 128), col(0), OP.is_gt)
-        tt(v("TRI"), v("TMPC"), v("BO"), OP.mult)
-        ts(col(14), col(0), 16.0, OP.mult)
-        ts(v("DLP"), v("AI", 0, 16), col(14), OP.add, 272.0, OP.add)
-        ts(v("FOUR"), v("DLP"), 272.0 + 254.0, OP.is_equal, 1600.0, OP.mult)
-        ts(v("FOUR"), v("FOUR"), 4.0, OP.add)
-        fill(v("ZERO"), 0.0)
-        fill(v("CE", 0, 1), 0.0)
-        fill(v("SC", 0, 1), 0.0)
-
-    def setup_d():
-        ts(v("MASK"), v("AI"), col(0), OP.is_equal)
-        ts(PA, PIX, 1, OP.add)
-        ts(PG, PA, 15, OP.bitwise_and)
-        ts(col(4), PG, 2.0, OP.mult)
-        ts(v("BO300"), v("BO"), 300.0, OP.mult)
-        ts(v("DC0"), v("CL0"), col(0), OP.add, float(S), OP.add)
-        ts(v("DC1"), v("DC0"), float(AREA), OP.add)
-        ts(v("DC2"), v("DC0"), float(DL - S), OP.add)
-        for i in "012":
-            ts(v("DD" + i), v("DC" + i), 1.0, OP.add)
-        fill(v("C255"), 255.0)
-        fill(v("ONE"), 1.0)
-        fill(v("RESP"), 0.0)
-
-    def hash_a(z, zc, n):
-        m = min(n, 128)
-        nb = (n + 127) // 128
-        for b in range(nb):
+    def hashes(terms, outs):
+        for b in (0, 1):
             for i in (0, 1):
-                mm(v("pUV", 16 * i + 8 * b, 16 * i + 8 * b + 8, p=m), v(z, zc + 128 * b, zc + 128 * b + m), v("WU", 8 * i, 8 * i + 8))
-        mm(v("pS", 0, n), v("WK"), v(z, zc, zc + n), True, False)
-        cp(v("UVI", p=m), v("pUV", 0, 32, p=m))
-        ts(v("UVM", p=m), v("UVI", p=m), 2047, OP.bitwise_and)
-        tt(v("TT", p=m), v("UVM", 0, 16, p=m), v("UVM", 16, 32, p=m), OP.mult)
-        k = 8 * nb
-        ts(v("TSI", 0, 16 * k, 16, p=m), v("TT", 0, k, p=m), 5, OP.arith_shift_right, 2047, OP.bitwise_and)
-        scan(v("TXF", 0, 16 * k, p=m), v("KEEP", 0, 16 * k, p=m), v("TSI", 0, 16 * k, p=m), OP.mult, OP.add)
-        for b in range(nb):
-            mm(v("pS", 128 * b, 128 * b + m), v("TXF", 128 * b, 128 * b + 128, p=m), v("IDH", 0, m, p=m), False, b == nb - 1)
+                for j, (z, zc, w, n) in enumerate(terms):
+                    mm(v("pB", 16 * i + 8 * b, 16 * i + 8 * b + 8), v(z, zc + 128 * b, zc + 128 * b + 128), v(w, 8 * i, 8 * i + 8), j == 0, j == len(terms) - 1)
+        mm(v("pS", 256, 512), v("HALF", p=1), v("ONE", p=1), True, False)
+        for h in (256, 0):
+            for z, zc, w, n in terms:
+                mm(v("pS", h, h + n), v(w, 16, 144), v(z, zc, zc + n), False, False)
+        cp(v("UVI"), v("pB", 0, 32))
+        ts(v("UVM"), v("UVI"), 2047, OP.bitwise_and)
+        tt(v("TT"), v("UVM", 0, 16), v("UVM", 16, 32), OP.mult)
+        ts(v("TSI", 0, 256, 16), v("TT"), 5, OP.arith_shift_right, 2047, OP.bitwise_and)
+        scan(v("TXF"), K256, v("TSI"), OP.mult, OP.add)
+        for h in (256, 0):
+            for b in (0, 1):
+                mm(v("pS", h + 128 * b, h + 128 * b + 128), v("TXF", 128 * b, 128 * b + 128), v("IDB"), False, h == 0 and b == 1)
+        for out, c0, c1 in outs:
+            ts(v("Y", c0, c1), v("pS", 256 + c0, 256 + c1), ROUND, OP.add, -ROUND, OP.add)
+            tt(v(out, c0, c1), v("pS", c0, c1), v("Y", c0, c1), OP.subtract)
 
-    def hash_b(n):
-        cp(v("HI", 0, n), v("pS", 0, n))
-        ts(v("HM", 0, n), v("HI", 0, n), 2047, OP.bitwise_and)
-        cp(v("H16", 0, n), v("HM", 0, n))
-
-    def expand(k0, k1):
-        scan(v("ZX", 16 * k0, 16 * k1), v("KEEP", 0, 16 * (k1 - k0)), v("ZS", 16 * k0, 16 * k1), OP.mult, OP.add)
-
-    def dist(cuts, n, hooks):
-        for i, (k0, k1) in enumerate(cuts):
-            x = v("DF", 16 * k0, 16 * k1)
-            tt(x, ind(v("U", 0, S), v("H16", k0, k1)), v("ZX", 16 * k0, 16 * k1), OP.subtract)
+    def dist(cuts, h, zx, df):
+        mm(v("pD", 0, 256), v("ONE", 0, 128, p=1), v("M2", p=1), True, False)
+        for k0, k1 in zip(cuts, cuts[1:]):
+            x = v(df, 16 * k0, 16 * k1)
+            tt(x, ind(v("U", 0, S), v(h, k0, k1)), v(zx, 16 * k0, 16 * k1), OP.subtract)
             act(x, x, AF.Abs)
-            for h in hooks.get(i, ()):
-                h()
             for r in range(k0 // 16, k1 // 16):
-                mm(v("pD", 0, 256), sel("S16", r), v("DF", 256 * r, 256 * r + 256), r == 0, r == n // 16 - 1)
-        for h in hooks.get("tail", ()):
-            h()
-        scan(v("KY"), v("RST"), v("pD", 0, 256), OP.add, OP.min)
+                mm(v("pD", 0, 256), sel("S16", r), v(df, 256 * r, 256 * r + 256), False, r == cuts[-1] // 16 - 1)
+        scan(v("KY"), v("R0"), v("pD", 0, 256), OP.max, OP.min, -1048576.0)
 
     KEY = v("KY", 15, 256, 16)
 
-    def choose(n, own, dc, lst, hook):
+    def choose(n, own, hm, dc, lst):
         k = n // 16
-        ts(v("PQ"), KEY, v("THR"), OP.is_ge)
+        ts(v("MC"), KEY, 31, OP.bitwise_and)
         if own:
-            tt(v("XN"), v("PQ"), v("NN"), OP.mult)
-            scan(v("SC", 1, 17), v("XN"), v("ZERO"), OP.add, OP.add)
-            mm(v("pX", 16, 17), v("TRI"), v("SC", 16, 17))
-        ts(v("MC"), KEY, 30, OP.bitwise_and)
-        if own:
-            tt(v("NE"), v("PQ"), v("NZ"), OP.max)
-        tt(v("CODE"), v("NE") if own else v("PQ"), v("MC"), OP.add)
-        for r in range(k):
-            mm(v("pC", 16 * r, 16 * r + 16), srow(r), v("CODE"))
-        hook()
+            tt(v("CODE"), v("MC"), v("NZ"), OP.add)
+        else:
+            cp(v("CODE"), v("MC"))
+        spread("pC", 0, v("CODE"), k)
         ts(v("OH", 0, n), v("pC", 0, n), col(4), OP.is_equal)
-        tt(v("HO", 0, n), v("OH", 0, n), v("HM", 0, n), OP.mult)
-        h1 = v("pC", 256, 256 + n)
-        mm(h1, v("BOH"), v("OH", 0, n), True, False)
-        mm(h1, v("BOH"), v("HO", 0, n), False, True)
-        mm(v("pN", 0, n), v("BO300"), v("OH", 0, n), True, False)
-        tt(v("M1", 0, n), h1, v("MASK", 0, n), OP.mult)
-        cp(v("HR", 0, n), h1)
-        scan(v("LS", 0, n), v("KEEP", 0, n), v("M1", 0, n), OP.mult, OP.add)
+        tt(v("HO", 0, n), v("OH", 0, n), v(hm, 0, n), OP.mult)
+        h1, h2, cnt = v("pH", 0, n), v("pC", 256, 256 + n), v("pN", 0, n)
+        mm(h2, v("IDB"), v("MB", 0, n), True, False)
+        mm(h2, v("BO"), v("HO", 0, n), False, True)
+        mm(h1, v("BO"), v("HO", 0, n))
+        mm(cnt, v("IDB"), v("MB", 0, n), True, False)
+        mm(cnt, v("NEG", p=1), v("ONE", 0, n, p=1), False, False)
+        mm(cnt, v("BON"), v("OH", 0, n), False, False)
+        mm(cnt, v("BO"), v("HO", 0, n), False, False)
+        scan(v("LS", 0, n), v("RST", 0, n), h2, OP.add, OP.min)
+        if own:
+            cp(v("HR"), h1)
         tt(v("EI", 0, n), h1, v("LS", 0, n), OP.is_equal)
-        mm(v("pN", 0, n), v("BO"), v("EI", 0, n), False, False)
-        kv = 11 if own else k - 1
+        mm(cnt, v("BO4"), v("EI", 0, n), False, False)
+        kv = min(KV, k - 1)
         o = [0]
         for c in range(k - 1):
             o.append(o[c] + n - 16 * (c + 1))
         for c in range(kv, k - 1):
-            act(v("EA", o[c] - o[kv], o[c + 1] - o[kv]), v("pC", 256 + 16 * (c + 1), 256 + n), AF.Abs, -1.0, v("LS", 16 * c + 15, 16 * c + 16))
+            act(v("EA", o[c] - o[kv], o[c + 1] - o[kv]), v("pH", 16 * (c + 1), n), AF.Abs, -1.0, v("LS", 16 * c + 15, 16 * c + 16))
         if kv < k - 1:
             act(v("EB", o[kv], o[k - 1]), v("EA", 0, o[k - 1] - o[kv]), AF.Relu, -1.0, 1.0)
         for c in range(k - 1):
             if c < kv:
-                ts(v("EB", o[c], o[c + 1]), v("HR", 16 * (c + 1), n), v("LS", 16 * c + 15, 16 * c + 16), OP.is_equal)
-            mm(v("pN", 16 * (c + 1), n), v("BO"), v("EB", o[c], o[c + 1]), False, c == k - 2)
-        HL = v("LS", 15, n, 16)
-        tt(v("HD", 0, k), HL, v("DD" + dc[2], 0, k), OP.subtract)
-        tt(v("CM", 0, n), v("pN", 0, n), v("MASK", 0, n), OP.mult)
-        scan(v("CS", 0, n), v("KEEP", 0, n), v("CM", 0, n), OP.mult, OP.add)
-        ts(v("WA", 0, k), v("CS", 15, n, 16), 301.0, OP.is_equal)
-        tt(v("WM", 0, k), v("WA", 0, k), v("HD", 0, k), OP.mult)
-        tt(v(lst, 0, k), v("WM", 0, k), v(dc, 0, k), OP.add)
+                ts(v("EB", o[c], o[c + 1]), v("HR" if own else "pH", 16 * (c + 1), n), v("LS", 16 * c + 15, 16 * c + 16), OP.is_equal)
+            mm(v("pN", 16 * (c + 1), n), v("BO4"), v("EB", o[c], o[c + 1]), False, c == k - 2)
+        scan(v("CS", 0, n), v("RST", 0, n), cnt, OP.add, OP.min)
+        tt(v(lst, 0, k), v("CS", 15, n, 16), v(dc, 0, k), OP.min)
 
     def numbers(A):
         for r in range(16):
-            mm(v("pM", 272, 288), sel("SN", r), v("NW", A + 16 * r, A + 16 * r + 16), r == 0, r == 15)
+            mm(v("pX", 0, 16), sel("SN", r), v("NW", A + 16 * r, A + 16 * r + 16), r == 0, r == 15)
 
     def put_course(t):
-        act(v("CF", 16 * t, 16 * t + 16), v("pM", 272, 288))
+        act(v("CF", 16 * t, 16 * t + 16), v("pX", 0, 16))
         dma("S", T.yc[:, 256 * t:256 * t + 256], v("CF", 16 * t, 16 * t + 16))
 
-    def widths(t):
+    def slots(t):
         if t:
-            cp(v("CI"), v("pM", 272, 288))
+            cp(v("CI"), v("pX", 0, 16))
         ts(v("CW"), v("CI") if t else v("C0L"), 3, OP.bitwise_and)
         scan(v("CE", 1, 17), v("CW"), v("FOUR"), OP.add, OP.add)
         mm(v("pX", 16, 17), v("TRI"), v("CE", 16, 17))
         ts(v("CFI", 0, 17), v("CE", 0, 17), v("pX", 16, 17), OP.add, 0.2, OP.mult)
         ts(v("F1", 0, 17), v("CFI", 0, 17), 256.0, OP.min)
         tt(v("NN"), v("F1", 1, 17), v("F1", 0, 16), OP.subtract)
-        ts(v("NZ"), v("NN"), 0.0, OP.is_equal)
+        tt(v("NZ"), v("F1", 1, 17), v("F1", 0, 16), OP.is_equal)
+        spread("pA", 256, v("F1", 0, 16))
+        act(v("F0R", 0, 256), v("pA", 256, 512))
+        for k in range(16):
+            lo, hi = 11 * k, min(L, 20 * k + 20)
+            act(v("JUNK", 0, hi - lo), v("F0R", lo, hi), AF.Sign, -1.0, v("IB", k, k + 1), v("JC", k, k + 1))
+        tt(v("JN", 1, 17), v("JC"), v("KC"), OP.add)
+        mm(v("pX", 32, 48), v("DM"), v("JN", 1, 17), True, False)
+        mm(v("pX", 32, 48), sel("S15", 0), v("JN", 0, 16), False, True)
+        mm(v("pX", 48, 64), v("HID"), v("JN", 1, 17))
+        ts(v("JF"), v("pX", 32, 48), 0.5, OP.is_ge, 256.0, OP.mult)
+        tt(v("SLOT"), v("pX", 48, 64), v("JF"), OP.add)
 
-    def slots_a():
-        for r in range(16):
-            mm(v("pM", 16 * r, 16 * r + 16), srow(r), v("F1", 0, 16))
-        act(v("F0R"), v("pM", 0, 256))
-        tt(v("DZ"), v("NZ"), v("DLP"), OP.mult)
-        tt(v("PF"), v("DZ"), v("F1", 0, 16), OP.add)
-        flip(v("PF"), None, v("JL"))
+    def asking():
+        ts(v("PQ"), KEY, v("THR"), OP.is_ge)
+        tt(v("XN"), v("PQ"), v("NN"), OP.mult)
+        spread("pH", 256, v("XN"))
+        scan(v("CUM", 1, 257), v("ONE"), v("pH", 256, 512), OP.mult, OP.add)
+        for k in range(3):
+            act(v("JUNK"), v("CUM", 1, 257), AF.Sign, -1.0, v("IB", k, k + 1), v("CNT", k, k + 1))
+        ts(v("LST"), v("CNT"), 0.5, OP.mult, 128.0, OP.add)
 
-    def slots_b():
-        cp(ind(v("J0"), v("JL")), v("CI1"))
-        scan(v("JM"), v("J0", 0, 256), v("J0", 0, 256), OP.max, OP.max)
-        act(v("JF"), v("J0", 0, 256), AF.Sign)
-
-    def slots_m():
-        for b, x in (("S0", "JM"), ("S256", "JF")):
+    def asker_slots():
+        act(v("GA"), ind(v("F0R"), v("LST", 0, 3)))
+        act(v("GB"), ind(v("CUM"), v("LST", 0, 3)))
+        mm(v("pX", 64, 67), v("IDB"), v("SI", 0, 3), True, False)
+        for b, x in (("S0", "GA"), ("S0N", "GB")):
             for p in range(16):
-                mm(v("pM", 256, 272), sel(b, p), v(x, p, 256, 16), b == "S0" and p == 0, b == "S256" and p == 15)
+                mm(v("pX", 64, 67), sel(b, p), v(x, p, CAP, 16), False, b == "S0N" and p == 15)
 
-    def slots_c():
-        cp(ind(v("SLW"), v("APL")), v("F0R"))
-        tt(v("SLM"), v("SLW", 0, CAP), v("MASK", 0, CAP), OP.mult)
-        scan(v("SLS"), v("KEEP", 0, CAP), v("SLM"), OP.mult, OP.add)
+    def bound():
+        act(v("R0", 0, 256, 16), AI16, AF.Identity, 0.0, v("THR"))
 
+    bound()
     for t in range(RO):
-        A = S + AREA * (t % 2)
-        B = S + AREA * (1 - t % 2)
+        A = A0 + AREA * (t % 2)
+        B = A0 + AREA * (1 - t % 2)
         lender = cores[(rank + 1 + t % (N - 1)) % N]
         asker = cores[(rank - 1 - t % (N - 1)) % N]
-        mm(v("pZ", 0, 256), v("PAM"), v("TW", A, A + L), True, False)
-        mm(v("pZ", 0, 255), v("PBM"), v("TW", A + 1, A + L), False, True)
-        cp(v("ZB"), v("pZ", 0, 256))
-        for m in range(16):
-            act(v("ZX", 1536 + m, 4096, 16), v("ZB", 96, 256))
-        cp(v("ZS", 0, 1536, 16), v("ZB", 0, 96))
-        hash_a("ZB", 0, 256)
-        if t == 0:
-            setup_b()
-        else:
+        last = t == RO - 1
+        hashes([("TW", A, "WL", 256), ("TW", A + 1, "WR", 256)], [("H16", 0, 64), ("H16", 64, 256)])
+        mm(v("pA", 0, 256), v("PAM"), v("TW", A, A + L), True, False)
+        mm(v("pA", 0, 256), v("PBM"), v("TW", A + 1, A + L + 1), False, True)
+        act(v("ZB"), v("pA", 0, 256))
+        z = WIN * t
+        message("z", t, lender, asker, v("ZL", z, z + 256), v("ZB"))
+        cp(v("ZS", 0, 16 * VX, 16), v("ZB", 0, VX))
+        scan(v("ZX", 0, 16 * VX), v("KEEP", 0, 16 * VX), v("ZS", 0, 16 * VX), OP.mult, OP.add)
+        for k0, k1 in zip(AX, AX[1:]):
+            for m in range(16):
+                act(v("ZX", 16 * k0 + m, 16 * k1, 16), v("ZB", k0, k1))
+        ts(v("HM"), v("H16"), 1.0, OP.add)
+        if t:
             cp(ind(v("NW", A, A + AREA), v("FIX", 0, 3)), v("NB", CAP * (t - 1), CAP * t))
             numbers(A)
-        expand(0, 64)
-        hash_b(256)
-
-        def course():
-            expand(64, 96)
-            if t == 0:
-                setup_c()
-            widths(t)
-            if t:
-                put_course(t - 1)
-        dist(CUTS, 256, {0: [course], "tail": [setup_d] * (t == 0) + [slots_a]})
-
-        def ask():
-            ts(v("E2"), v("XN"), 0.0, OP.is_equal)
-            tt(v("E2"), v("E2"), v("DLP"), OP.mult)
-            tt(v("SX"), v("SC", 0, 16), v("E2"), OP.add)
-            flip(v("SX"), v("pX", 16, 17), v("APL"))
-            cp(ind(v("ASKW"), v("APL")), v("ZB"))
-            send(lender, v("ASKL", CAP * t, CAP * t + CAP), v("ASKW", 0, CAP), "aa%d" % t, "la%d" % t)
-            arrives(v("ASKL", CAP * t, CAP * t + CAP), asker, "aa%d" % t)
-        choose(256, True, "DC%d" % (t % 2), "LAY", ask)
-        cp(ind(v("U", 0, DL), v("LAY")), v("C255"))
-        if t < RO - 1:
+            put_course(t - 1)
+        slots(t)
+        dist(CUTS, "H16", "ZX", "DF")
+        asking()
+        message("q", t, lender, asker, v("LSL", 8 * t, 8 * t + 4), v("LST"))
+        hashes([("ZL", z, "WA", 256)], [("HL", 0, 256)])
+        choose(256, True, "HM", "DC%d" % (t % 2), "LAY")
+        cp(ind(v("U"), v("LAY")), v("C255"))
+        if not last:
             act(v("TW", A + L, A + 2 * L), ind(v("TW", 0, A + L), v("LAY")))
-        act(v("NW", A + L, A + 2 * L), ind(v("NW", 0, A + L), v("LAY")))
-        z = CAP * t
-        hash_a("ASKL", z, CAP)
-        cp(v("ZS", 0, 16 * CAP, 16), v("ASKL", z, z + CAP))
-        expand(0, CAP)
-        hash_b(CAP)
-        dist([(0, 32), (32, 48)], CAP, {"tail": [slots_b]})
-        choose(CAP, False, "DC2", "LEN", lambda: None)
-        slots_m()
-        act(v("RESP", 48, 96), ind(v("TW"), v("LEN", 0, 3)))
-        cp(v("RESP", 0, 48), ind(v("U"), v("LEN", 0, 3)))
-        ts(v("RESP", 96, 99), v("LEN", 0, 3), float(DL), OP.is_ge, 256.0, OP.mult)
-        send(asker, v("RETL", RETN * t, RETN * t + RETN), v("RESP"), "ar%d" % t, "lr%d" % t)
-        arrives(v("RETL", RETN * t, RETN * t + RETN), lender, "ar%d" % t)
-        slots_c()
-        ts(v("SLOT"), v("pM", 256, 272), -1.0, OP.add)
-        cp(ind(v("U"), v("LEN", 0, 3)), v("C255", 0, 48))
-        if t < RO - 1:
             act(v("TW", B, B + L), ind(v("TW", A, A + 2 * L), v("SLOT")))
+        act(v("NW", A + L, A + 2 * L), ind(v("NW", 0, A + L), v("LAY")))
         act(v("NW", B, B + L), ind(v("NW", A, A + 2 * L), v("SLOT")))
-        if t < RO - 1:
-            act(v("U", DL, WID), v("KEEP", 0, CAP), scale=0.0)
-            prefill()
-            mm(v("pX", 18, 19), v("ONE"), v("SC", 16, 17))
+        asker_slots()
+        lst = v("LSL", 8 * t, 8 * t + 3)
+        cp(v("H16L"), ind(v("HL"), lst))
+        cp(v("ZSL", 0, 768, 16), ind(v("ZL", z, z + WIN), lst))
+        scan(v("ZXL"), v("KEEP", 0, 768), v("ZSL"), OP.mult, OP.add)
+        ts(v("HML"), v("H16L"), 1.0, OP.add)
+        act(v("U", DL, DL + CAP), v("AI", 0, CAP), scale=0.0)
+        dist([0, 32, 48], "H16L", "ZXL", "DFL")
+        choose(CAP, False, "HML", "DC2", "LEN")
+        r0 = RETN * t
+        ts(v("RESP", 48, 51), v("CS", 15, CAP, 16), float(S), OP.is_ge, 256.0, OP.mult)
+        if last:
+            message("a", t, asker, lender, v("RETL", r0 + 48, r0 + RETN), v("RESP", 48, RETN))
+        else:
+            cp(v("RESP", 0, 48), ind(v("TW", 0, A0), v("LEN", 0, 3)))
+            message("a", t, asker, lender, v("RETL", r0, r0 + RETN), v("RESP"))
+        act(v("RESU"), ind(v("U", 0, A0), v("LEN", 0, 3)))
+        message("u", t, asker, lender, v("UB", CAP * t, CAP * t + CAP), v("RESU"))
+        cp(ind(v("U", 0, A0), v("LEN", 0, 3)), v("C255", 0, 48))
+        if not last:
+            mm(v("pX", 18, 19), v("E0"), v("CUM", 256, 257))
             cp(v("PIN"), v("pX", 18, 19))
             ts(v("PI2"), v("PIN"), 63, OP.bitwise_and)
-            ts(v("THR"), v("PI2"), 32.0, OP.mult, v("TH16"), OP.add)
-        r0 = RETN * t
-        tt(v("FIX", 0, 3), v("SLS", 15, CAP, 16), v("RETL", r0 + 96, r0 + 99), OP.add)
-        if t < RO - 1:
-            cp(ind(v("TW", B, B + AREA), v("FIX", 0, 3)), v("RETL", r0 + 48, r0 + 96))
-        act(v("UB", CAP * t, CAP * t + CAP), v("RETL", r0, r0 + 48))
-    dma("S", T.yu[:, 0:S], v("U", 0, S))
-    B = S + AREA * (RO % 2)
+            ts(v("THR"), v("PI2"), 32.0, OP.mult, v("TH32"), OP.add)
+            bound()
+        tt(v("FIX", 0, 3), v("pX", 64, 67), v("RETL", r0 + 48, r0 + 51), OP.add)
+        if not last:
+            cp(ind(v("TW", B, B + AREA), v("FIX", 0, 3)), v("RETL", r0, r0 + 48))
+    dma("S", T.yu[:, 0:S], v("U", 0, S), 3 * NEAR)
+    B = A0 + AREA * (RO % 2)
     cp(ind(v("NW", B, B + AREA), v("FIX", 0, 3)), v("NB", CAP * (RO - 1), CAP * RO))
     numbers(B)
     put_course(RO - 1)
-    dma("S", T.yu[:, S:S + RO * CAP], v("UB"))
-    for s in ("sV", "sA", "sP", "sG"):
-        g.wait_ge(T.sem[s], count[s])
-    for i in range(ndma[0]):
-        g.sync.wait_ge(T.sem["d%d" % i], 16)
-    for t in range(RO):
-        lender = cores[(rank + 1 + t % (N - 1)) % N]
-        asker = cores[(rank - 1 - t % (N - 1)) % N]
-        for s, n in (("la", len(engs(core, lender))), ("lr", len(engs(core, asker))), ("aa", len(engs(asker, core))), ("ar", len(engs(lender, core)))):
-            g.wait_ge(T.sem[s + str(t)], n)
+    dma("A", T.yu[:, S:S + RO * CAP], v("UB"))
+
+    n = len(ops)
+    nxt = [[] for _ in ops]
+    for i, o in enumerate(ops):
+        for j in o["pre"] | o["after"]:
+            nxt[j].append(i)
+
+    def gap(j, i):
+        return 0 if ops[i]["q"] == "N" or ops[j]["q"] == ops[i]["q"] == "P" else WAKE
+    tail = [0] * n
+    for i in range(n - 1, -1, -1):
+        tail[i] = ops[i]["dur"] + ops[i]["lat"] + max([gap(i, j) + tail[j] for j in nxt[i]] + [0])
+    left = [len(o["pre"] | o["after"]) for o in ops]
+    ready = {i: 0 for i in range(n) if not left[i]}
+    free = {q: 0 for q in "VAPGSN"}
+    used = {b: {} for b in _ps}
+    end = [0] * n
+    order = []
+
+    def begin(i):
+        o = ops[i]
+        return max([free[o["q"]], ready[i]] + [e + WAKE for b in o["banks"] for q, e in used[b].items() if q != o["q"]])
+    while ready:
+        start = {i: begin(i) for i in ready}
+        first = min(ready, key=lambda i: (start[i] + ops[i]["dur"], i))
+        q, by = ops[first]["q"], start[first] + ops[first]["dur"]
+        i = max((j for j in ready if ops[j]["q"] == q and (start[j] < by or j == first)), key=lambda j: (tail[j], -j))
+        o = ops[i]
+        if q != "N":
+            free[q] = start[i] + o["dur"]
+        end[i] = start[i] + o["dur"] + o["lat"]
+        for b in o["banks"]:
+            used[b][q] = end[i]
+        del ready[i]
+        order.append(i)
+        for j in nxt[i]:
+            left[j] -= 1
+            if not left[j]:
+                ready[j] = max(end[k] + gap(k, j) for k in ops[j]["pre"] | ops[j]["after"])
+
+    count = {"V": 0, "A": 0, "P": 0, "G": 0}
+    know = {q: {} for q in Q}
+    token, snap = {}, {}
+    touched = {b: {} for b in _ps}
+    for i in order:
+        o = ops[i]
+        q = o["q"]
+        if q == "N":
+            token[i] = o["own"]
+            continue
+        deps = [token[j] for j in o["pre"] if not ops[j]["q"] == q == "P"]
+        deps += [tk for b in o["banks"] for e, tk in touched[b].items() if e != q]
+        want = {}
+        for s, val in deps:
+            want[s] = max(want.get(s, 0), val)
+        k = know[q]
+        for s in sorted(want, key=lambda s: -len(snap.get((s, want[s]), ()))):
+            if k.get(s, 0) < want[s]:
+                Q[q].wait_ge(T.sem[s], want[s])
+                k[s] = want[s]
+                for s2, v2 in snap.get((s, want[s]), {}).items():
+                    k[s2] = max(k.get(s2, 0), v2)
+        if o["own"]:
+            o["f"]()
+            token[i] = o["own"]
+        else:
+            count[q] += 1
+            o["f"]().then_inc(T.sem["s" + q], 1)
+            token[i] = ("s" + q, count[q])
+        snap[token[i]] = dict(k)
+        for b in o["banks"]:
+            touched[b][q] = token[i]
+    for q in count:
+        g.wait_ge(T.sem["s" + q], count[q])
+    for s in dmas:
+        g.sync.wait_ge(T.sem[s], 16)
+    for s, val in far:
+        g.wait_ge(T.sem[s], val)

@@ -18,7 +18,8 @@ _sb = {
     "GI": (128, "float32"), "YI": (144, "float32"), "AI": (256, "float32"),
     "BO": (128, "bfloat16"), "BO4": (128, "bfloat16"), "BON": (128, "bfloat16"), "IDB": (128, "bfloat16"), "SB": (144, "bfloat16"),
     "S16": (144, "bfloat16"), "SN": (144, "bfloat16"), "S0": (144, "bfloat16"), "S0N": (144, "bfloat16"), "S15": (144, "bfloat16"),
-    "SR": (2048, "bfloat16"), "PAM": (128, "bfloat16"), "PBM": (128, "bfloat16"), "HID": (128, "bfloat16"), "DM": (128, "bfloat16"),
+    "SR": (384, "bfloat16"), "SR2": (1024, "bfloat16"), "SEL2": (16, "float32"), "NN2": (32, "bfloat16"), "NZ2": (32, "float32"),
+    "F2": (32, "bfloat16"), "EL": (4, "uint16"), "REST": (CAP, "bfloat16"), "RESF": (8, "bfloat16"), "PAM": (128, "bfloat16"), "PBM": (128, "bfloat16"), "HID": (128, "bfloat16"), "DM": (128, "bfloat16"),
     "SHM": (128, "bfloat16"), "TRI": (128, "bfloat16"), "ONE": (256, "bfloat16"), "NEG": (128, "bfloat16"), "E0": (128, "bfloat16"),
     "HALF": (128, "float16"), "M2": (256, "bfloat16"), "MB": (256, "bfloat16"), "R0": (256, "float32"), "RST": (256, "float32"),
     "KEEP": (1024, "bfloat16"), "CL0": (16, "float32"), "DC0": (16, "float32"), "DC1": (16, "float32"), "DC2": (16, "float32"),
@@ -32,15 +33,15 @@ _sb = {
     "HL": (WIN, "int32"), "H16L": (48, "uint16"), "HML": (48, "float16"),
     "ZS": (1024, "bfloat16"), "ZX": (4096, "bfloat16"), "DF": (4096, "bfloat16"), "KY": (256, "int32"),
     "ZSL": (768, "bfloat16"), "ZXL": (768, "bfloat16"), "DFL": (768, "bfloat16"),
-    "PQ": (16, "bfloat16"), "XN": (16, "bfloat16"), "CUM": (WIN, "bfloat16"), "CNT": (4, "float32"), "LST": (4, "uint16"),
-    "JUNK": (256, "bfloat16"), "GA": (48, "bfloat16"), "GB": (48, "bfloat16"), "PIN": (1, "int32"), "PI2": (1, "int32"),
-    "MC": (16, "int32"), "CODE": (16, "bfloat16"), "OH": (256, "float16"), "HO": (256, "float16"),
-    "HR": (256, "float16"), "LS": (256, "float32"), "EI": (256, "bfloat16"), "EB": (1920, "bfloat16"), "EA": (336, "float32"),
+    "PQ": (16, "bfloat16"), "XN": (32, "bfloat16"), "CUM": (WIN, "bfloat16"), "CNT": (4, "float32"), "LST": (4, "uint16"),
+    "JUNK": (2816, "bfloat16"), "NID": (128, "bfloat16"), "Y1": (256, "float32"), "ZA": (48, "bfloat16"), "GA": (48, "bfloat16"), "GB": (48, "bfloat16"), "PIN": (1, "int32"), "PI2": (1, "int32"),
+    "MC": (16, "int32"), "CODE": (32, "bfloat16"), "OH": (256, "float16"), "HO": (256, "float16"),
+    "HR": (256, "float16"), "LS": (256, "float32"), "EI": (256, "bfloat16"), "EB": (1920, "bfloat16"), "EA": (768, "float32"),
     "CS": (256, "float32"), "LAY": (16, "uint16"), "LEN": (4, "uint16"),
     "CI": (16, "int32"), "CW": (16, "int32"), "CE": (32, "bfloat16"), "CFI": (32, "int32"), "F1": (32, "bfloat16"),
     "NN": (16, "bfloat16"), "NZ": (16, "float32"), "F0R": (WIN, "bfloat16"), "JC": (16, "float32"), "JN": (32, "float16"),
     "JF": (16, "float32"), "SLOT": (16, "uint16"), "FIX": (4, "uint16"), "CF": (80, "float32"),
-    "ZL": (RO * WIN, "bfloat16"), "LSL": (RO * 8, "uint16"), "RESP": (RETN, "bfloat16"), "RESU": (CAP, "bfloat16"),
+    "ZL": (RO * WIN, "bfloat16"), "LSL": (RO * 8, "uint16"), "RESU": (CAP, "bfloat16"),
     "RETL": (RO * RETN, "bfloat16"), "UB": (240, "bfloat16"),
 }
 _ps = ("pA", "pB", "pS", "pD", "pC", "pH", "pN", "pX")
@@ -55,13 +56,75 @@ SCRATCH = {k: ("sbuf", [128, _sb[k][0]], _sb[k][1]) for k in _sb if k not in _pl
 SCRATCH.update({"pack_" + k: ("sbuf", [128, _fill[k]], k) for k in _fill})
 SCRATCH.update({k: ("psum", [128, 512], "float32") for k in _ps})
 _bytes = {"bfloat16": 2, "float16": 2, "uint16": 2, "float32": 4, "int32": 4}
-MSG = ("z", "q", "a", "u")
+MSG = ("z", "q", "t", "a", "u")
 SEMAPHORES = ["sV", "sA", "sP", "sG"] + ["d%d" % i for i in range(16)] + [e + m + str(t) for e in "lr" for m in MSG for t in range(RO)]
-CUTS = [0, 32, 64, 96, 128, 160, 192, 224, 240, 256]
-VX = 64
-AX = [64, 160, 256]
-KV = 12
+OWN = [(0, 32, None), (96, 128, None), (32, 64, "pC"), (128, 160, None), (64, 96, "pH"), (160, 192, None), (192, 224, None),
+       (224, 240, None), (240, 256, None)]
+LENT = [(0, 16, None), (32, 48, "pC"), (16, 32, None)]
+COPIES = [("V", 0, 32), ("A", 96, 192), ("G", 192, 256)]
+TURNS, STEPS = 3, (0, 200)
+EARLY = 2000
+ZEARLY = 6000
+EIAT = 6
+HCUT = 96
+KV = 11
 LEAST, WAKE, GATHER, SCATTER, FAR, NEAR = 64, 140, 1.5, 3.5, 2600, 1600
+
+
+_once = {}
+
+
+def issue_order(ops):
+    n = len(ops)
+    pre = [{j: ops[j]["lat"] + (0 if o["q"] == "N" or o["q"] == ops[j]["q"] == "P" else WAKE) for j in o["pre"] | o["after"]} for o in ops]
+    nxt = [{} for _ in ops]
+    for i in range(n):
+        for j in pre[i]:
+            nxt[j][i] = pre[i][j] + ops[j].get("early", 0)
+
+    def place(seq, before, back):
+        end = [0] * n
+        line = {}
+        for i in seq:
+            o = ops[i]
+            q, d = o["q"], o["dur"]
+            t = max([end[j] + w for j, w in before[i].items()] + [o["lat"] if back else 0])
+            lines = [(line.setdefault(q, []), 0)] * (q != "N") + [(line.setdefault((b, e), []), WAKE) for b in o["banks"] for e in "VAP" if e != q]
+            moved = True
+            while moved:
+                moved = False
+                for taken, w in lines:
+                    k = seek(taken, t - w)
+                    while k < len(taken) and taken[k][0] < t + d + w:
+                        t, k, moved = taken[k][1] + w, k + 1, True
+            for key in [q] * (q != "N") + [(b, q) for b in o["banks"]]:
+                taken = line.setdefault(key, [])
+                taken.insert(seek(taken, t), (t, t + d))
+            end[i] = t + d
+        return end
+
+    def seek(taken, t):
+        lo, hi = 0, len(taken)
+        while lo < hi:
+            mid = (lo + hi) // 2
+            if taken[mid][1] > t:
+                hi = mid
+            else:
+                lo = mid + 1
+        return lo
+    best = None
+    for step in STEPS:
+        key = [0] * n
+        for i in range(n - 1, -1, -1):
+            key[i] = ops[i]["dur"] + max([w + step * (ops[j]["q"] in "VA") + key[j] for j, w in nxt[i].items()] + [ops[i]["lat"]])
+        for turn in range(TURNS):
+            end = place(sorted(range(n), key=lambda i: (-key[i], i)), pre, False)
+            total = max(end[i] + ops[i]["lat"] for i in range(n))
+            if best is None or total < best[0]:
+                best = (total, sorted(range(n), key=lambda i: (end[i] - ops[i]["dur"], end[i], i)), step, turn)
+            key = place(sorted(range(n), key=lambda i: (-end[i], -i)), nxt, True)
+    _once["best"] = (best[0], best[2], best[3])
+    return best[1]
 
 
 def rank_program(g, core, T, topo):
@@ -187,10 +250,13 @@ def rank_program(g, core, T, topo):
                 65 + GATHER * n if in_[0] == "I" else max(LEAST, n))
         else:
             add("A", total, [in_, scale, bias], lambda: g.scalar.activation(out=ap(out), in_=ap(in_), func=func, bias=ap(bias), scale=ap(scale),
-                                                                            accum_out=ap(total)), max(LEAST, n) + 20, after=dumps[-1:])
-            ops[-1]["pre"].update(dumps[-1:])
-            dumps.append(len(ops) - 1)
-    dumps = []
+                                                                            accum_out=ap(total)), max(LEAST, n) + 20)
+            ops[-1]["pre"].update(dumps.get(out, []))
+            dumps[out] = [len(ops) - 1]
+    dumps = {}
+
+    def gcp(out, in_):
+        add("G", out, [in_], lambda: g.affine_select(ap(out), ap(in_), [[0, size(out)]], OP.is_ge, 0.0, 0, 0), 170 + 2 * size(out))
 
     def mm(out, lhsT, rhs, start=True, stop=True):
         add("P", out, [lhsT, rhs], lambda: g.tensor.matmul(ap(out), ap(lhsT), ap(rhs), start=start, stop=stop),
@@ -267,6 +333,9 @@ def rank_program(g, core, T, topo):
     ts(col(16), v("PA_"), 15.0, OP.is_lt, -0.5, OP.mult)
     ts(col(17), PIX, 1.0, OP.add)
     ts(col(18), v("PA_"), 2.0, OP.is_lt)
+    ts(v("PC_"), PIX, 1, OP.bitwise_and)
+    ts(col(19), v("PC_"), 0.0, OP.is_equal)
+    cp(col(20), v("PC_"))
     ts(col(13), col(11), 15.0, OP.mult, col(18), OP.add)
     ts(v("BO"), GI, col(1), OP.is_equal)
     ts(v("SELC"), AI16, col(0), OP.is_equal)
@@ -284,8 +353,8 @@ def rank_program(g, core, T, topo):
             act((out[0], j, j + n, 1, 128), v("AI", 0, n), scale=0.0, bias=c)
     const(v("ONE"), 1.0)
     const(v("NEG"), -1.0)
-    const(v("ZS"), 0.0)
-    const(v("ZSL"), 0.0)
+    fill(v("ZS"), 0.0)
+    fill(v("ZSL"), 0.0)
     const(v("R0"), -1048576.0)
     const(v("C255"), 255.0)
     const(v("CUM", 0, 1), 0.0)
@@ -293,10 +362,10 @@ def rank_program(g, core, T, topo):
     const(v("F0R", 256, WIN), 256.0)
     const(v("CE", 0, 1), 0.0)
     const(v("CNT", 3, 4), 0.0)
-    const(v("RESP", 48, RETN), 0.0)
+    const(v("RESF", 3, 8), 0.0)
     for b in ("U", "TW", "NW"):
         const(v(b, S, A0), 0.0)
-        const(v(b, A0 + (0 if b == "U" else L), WID), 0.0)
+        fill(v(b, A0 + (0 if b == "U" else L), WID), 0.0)
     for t in range(RO):
         const(v("ZL", WIN * t + 256, WIN * t + WIN), 1024.0)
     act(v("RST"), K256, scale=-1048576.0, bias=1048576.0)
@@ -307,11 +376,15 @@ def rank_program(g, core, T, topo):
     act(v("S0N"), v("SB"), scale=col(12))
     act(v("S15"), v("SB"), scale=col(15))
     act(v("HID"), v("IDB"), scale=0.5)
+    act(v("NID"), v("IDB"), scale=-1.0)
     act(v("BO4"), v("BO"), scale=BIG)
     act(v("BON"), v("BO"), scale=-BIG)
     act(v("E0"), v("ONE", 0, 128), scale=col(11))
-    for r in range(16):
+    tt(v("SEL2", 0, 8), v("SELC", 0, 16, 2), v("SELC", 1, 16, 2), OP.add)
+    for r in range(3):
         act(v("SR", 128 * r, 128 * r + 128), v("BO"), scale=v("SELC", r, r + 1))
+    for r in range(8):
+        act(v("SR2", 128 * r, 128 * r + 128), v("BO"), scale=v("SEL2", r, r + 1))
     fill(v("HL", 256, WIN), 0)
     fill(v("TSI"), 0)
     ts(v("HALF", p=32), v("GI", p=32), 0.0, OP.mult, -1023.5, OP.add)
@@ -359,39 +432,53 @@ def rank_program(g, core, T, topo):
     def sel(b, r):
         return v(b, 15 - r, 143 - r)
 
-    def spread(out, c0, x, k=16):
-        for r in range(k):
-            mm(v(out, c0 + 16 * r, c0 + 16 * r + 16), v("SR", 128 * r, 128 * r + 128), x)
+    def spread(out, c0, x):
+        for r in range(8):
+            mm(v(out, c0 + 32 * r, c0 + 32 * r + 32), v("SR2", 128 * r, 128 * r + 128), x)
 
     def hashes(terms, outs):
         for b in (0, 1):
             for i in (0, 1):
                 for j, (z, zc, w, n) in enumerate(terms):
                     mm(v("pB", 16 * i + 8 * b, 16 * i + 8 * b + 8), v(z, zc + 128 * b, zc + 128 * b + 128), v(w, 8 * i, 8 * i + 8), j == 0, j == len(terms) - 1)
-        mm(v("pS", 256, 512), v("HALF", p=1), v("ONE", p=1), True, False)
-        for h in (256, 0):
-            for z, zc, w, n in terms:
-                mm(v("pS", h, h + n), v(w, 16, 144), v(z, zc, zc + n), False, False)
+        mm(v("pD", 256, 512), v("HALF", p=1), v("ONE", p=1), True, False)
+        for bank, h in (("pD", 256), ("pS", 0)):
+            for j, (z, zc, w, n) in enumerate(terms):
+                mm(v(bank, h, h + n), v(w, 16, 144), v(z, zc, zc + n), h + j == 0, False)
         cp(v("UVI"), v("pB", 0, 32))
         ts(v("UVM"), v("UVI"), 2047, OP.bitwise_and)
         tt(v("TT"), v("UVM", 0, 16), v("UVM", 16, 32), OP.mult)
         ts(v("TSI", 0, 256, 16), v("TT"), 5, OP.arith_shift_right, 2047, OP.bitwise_and)
-        scan(v("TXF"), K256, v("TSI"), OP.mult, OP.add)
-        for h in (256, 0):
-            for b in (0, 1):
-                mm(v("pS", h + 128 * b, h + 128 * b + 128), v("TXF", 128 * b, 128 * b + 128), v("IDB"), False, h == 0 and b == 1)
+        for b in range(0, 256, 256 // len(terms)):
+            e = b + 256 // len(terms)
+            scan(v("TXF", b, e), v("KEEP", b, e), v("TSI", b, e), OP.mult, OP.add)
+        for b in (0, 1):
+            for bank, h in (("pD", 256), ("pS", 0)):
+                mm(v(bank, h + 128 * b, h + 128 * b + 128), v("TXF", 128 * b, 128 * b + 128), v("IDB"), False, b == 1)
         for out, c0, c1 in outs:
-            ts(v("Y", c0, c1), v("pS", 256 + c0, 256 + c1), ROUND, OP.add, -ROUND, OP.add)
+            if len(terms) > 1:
+                ts(v("Y", c0, c1), v("pD", 256 + c0, 256 + c1), ROUND, OP.add, -ROUND, OP.add)
+            else:
+                act(v("Y1", c0, c1), v("pD", 256 + c0, 256 + c1), bias=ROUND)
+                act(v("Y", c0, c1), v("Y1", c0, c1), bias=-ROUND)
             tt(v(out, c0, c1), v("pS", c0, c1), v("Y", c0, c1), OP.subtract)
 
-    def dist(cuts, h, zx, df):
+    def dist(pieces, h, z, zx, df):
         mm(v("pD", 0, 256), v("ONE", 0, 128, p=1), v("M2", p=1), True, False)
-        for k0, k1 in zip(cuts, cuts[1:]):
-            x = v(df, 16 * k0, 16 * k1)
-            tt(x, ind(v("U", 0, S), v(h, k0, k1)), v(zx, 16 * k0, 16 * k1), OP.subtract)
-            act(x, x, AF.Abs)
+        for k0, k1, bank in pieces:
+            x, stones = v(df, 16 * k0, 16 * k1), ind(v("U", 0, S), v(h, k0, k1))
+            if bank:
+                n = 16 * (k1 - k0)
+                for m in range(16):
+                    mm(v(bank, m, n, 16), v("NID"), v(z, k0, k1), m == 0, False)
+                act(x, stones)
+                mm(v(bank, 0, n), v("IDB"), x, False, True)
+                act(x, v(bank, 0, n), AF.Abs)
+            else:
+                tt(x, stones, v(zx, 16 * k0, 16 * k1), OP.subtract)
+                act(x, x, AF.Abs)
             for r in range(k0 // 16, k1 // 16):
-                mm(v("pD", 0, 256), sel("S16", r), v(df, 256 * r, 256 * r + 256), False, r == cuts[-1] // 16 - 1)
+                mm(v("pD", 0, 256), sel("S16", r), v(df, 256 * r, 256 * r + 256), False, k0 == pieces[-1][0] and r == k1 // 16 - 1)
         scan(v("KY"), v("R0"), v("pD", 0, 256), OP.max, OP.min, -1048576.0)
 
     KEY = v("KY", 15, 256, 16)
@@ -400,10 +487,13 @@ def rank_program(g, core, T, topo):
         k = n // 16
         ts(v("MC"), KEY, 31, OP.bitwise_and)
         if own:
-            tt(v("CODE"), v("MC"), v("NZ"), OP.add)
+            for j in (0, 16):
+                tt(v("CODE", j, j + 16), v("MC"), v("NZ2", j, j + 16), OP.min)
+            spread("pC", 0, v("CODE"))
         else:
-            cp(v("CODE"), v("MC"))
-        spread("pC", 0, v("CODE"), k)
+            cp(v("CODE", 0, 16), v("MC"))
+            for r in range(k):
+                mm(v("pC", 16 * r, 16 * r + 16), v("SR", 128 * r, 128 * r + 128), v("CODE", 0, 16))
         ts(v("OH", 0, n), v("pC", 0, n), col(4), OP.is_equal)
         tt(v("HO", 0, n), v("OH", 0, n), v(hm, 0, n), OP.mult)
         h1, h2, cnt = v("pH", 0, n), v("pC", 256, 256 + n), v("pN", 0, n)
@@ -418,7 +508,6 @@ def rank_program(g, core, T, topo):
         if own:
             cp(v("HR"), h1)
         tt(v("EI", 0, n), h1, v("LS", 0, n), OP.is_equal)
-        mm(cnt, v("BO4"), v("EI", 0, n), False, False)
         kv = min(KV, k - 1)
         o = [0]
         for c in range(k - 1):
@@ -430,6 +519,8 @@ def rank_program(g, core, T, topo):
         for c in range(k - 1):
             if c < kv:
                 ts(v("EB", o[c], o[c + 1]), v("HR" if own else "pH", 16 * (c + 1), n), v("LS", 16 * c + 15, 16 * c + 16), OP.is_equal)
+            if c == min(EIAT, k - 2):
+                mm(cnt, v("BO4"), v("EI", 0, n), False, False)
             mm(v("pN", 16 * (c + 1), n), v("BO4"), v("EB", o[c], o[c + 1]), False, c == k - 2)
         scan(v("CS", 0, n), v("RST", 0, n), cnt, OP.add, OP.min)
         tt(v(lst, 0, k), v("CS", 15, n, 16), v(dc, 0, k), OP.min)
@@ -451,12 +542,17 @@ def rank_program(g, core, T, topo):
         ts(v("CFI", 0, 17), v("CE", 0, 17), v("pX", 16, 17), OP.add, 0.2, OP.mult)
         ts(v("F1", 0, 17), v("CFI", 0, 17), 256.0, OP.min)
         tt(v("NN"), v("F1", 1, 17), v("F1", 0, 16), OP.subtract)
-        tt(v("NZ"), v("F1", 1, 17), v("F1", 0, 16), OP.is_equal)
-        spread("pA", 256, v("F1", 0, 16))
+        ops[-1]["early"] = EARLY
+        for j in (0, 1):
+            x = (16 * j, 16 * j + 16)
+            ts(v("NN2", *x), v("NN"), col(19 + j), OP.mult)
+            act(v("F2", *x), v("F1", 0, 16), scale=col(19 + j))
+            ts(v("NZ2", *x), v("NN2", *x), 32.0, OP.mult, col(19 + j), OP.subtract)
+        spread("pA", 256, v("F2"))
         act(v("F0R", 0, 256), v("pA", 256, 512))
         for k in range(16):
             lo, hi = 11 * k, min(L, 20 * k + 20)
-            act(v("JUNK", 0, hi - lo), v("F0R", lo, hi), AF.Sign, -1.0, v("IB", k, k + 1), v("JC", k, k + 1))
+            act(v("JUNK", 128 * k, 128 * k + hi - lo), v("F0R", lo, hi), AF.Sign, -1.0, v("IB", k, k + 1), v("JC", k, k + 1))
         tt(v("JN", 1, 17), v("JC"), v("KC"), OP.add)
         mm(v("pX", 32, 48), v("DM"), v("JN", 1, 17), True, False)
         mm(v("pX", 32, 48), sel("S15", 0), v("JN", 0, 16), False, True)
@@ -466,11 +562,12 @@ def rank_program(g, core, T, topo):
 
     def asking():
         ts(v("PQ"), KEY, v("THR"), OP.is_ge)
-        tt(v("XN"), v("PQ"), v("NN"), OP.mult)
+        for j in (0, 16):
+            tt(v("XN", j, j + 16), v("PQ"), v("NN2", j, j + 16), OP.mult)
         spread("pH", 256, v("XN"))
         scan(v("CUM", 1, 257), v("ONE"), v("pH", 256, 512), OP.mult, OP.add)
         for k in range(3):
-            act(v("JUNK"), v("CUM", 1, 257), AF.Sign, -1.0, v("IB", k, k + 1), v("CNT", k, k + 1))
+            act(v("JUNK", 2048 + 256 * k, 2304 + 256 * k), v("CUM", 1, 257), AF.Sign, -1.0, v("IB", k, k + 1), v("CNT", k, k + 1))
         ts(v("LST"), v("CNT"), 0.5, OP.mult, 128.0, OP.add)
 
     def asker_slots():
@@ -491,24 +588,29 @@ def rank_program(g, core, T, topo):
         lender = cores[(rank + 1 + t % (N - 1)) % N]
         asker = cores[(rank - 1 - t % (N - 1)) % N]
         last = t == RO - 1
-        hashes([("TW", A, "WL", 256), ("TW", A + 1, "WR", 256)], [("H16", 0, 64), ("H16", 64, 256)])
+        hashes([("TW", A, "WL", 256), ("TW", A + 1, "WR", 256)], [("H16", 0, HCUT), ("H16", HCUT, 256)])
         mm(v("pA", 0, 256), v("PAM"), v("TW", A, A + L), True, False)
         mm(v("pA", 0, 256), v("PBM"), v("TW", A + 1, A + L + 1), False, True)
         act(v("ZB"), v("pA", 0, 256))
         z = WIN * t
         message("z", t, lender, asker, v("ZL", z, z + 256), v("ZB"))
-        cp(v("ZS", 0, 16 * VX, 16), v("ZB", 0, VX))
-        scan(v("ZX", 0, 16 * VX), v("KEEP", 0, 16 * VX), v("ZS", 0, 16 * VX), OP.mult, OP.add)
-        for k0, k1 in zip(AX, AX[1:]):
-            for m in range(16):
-                act(v("ZX", 16 * k0 + m, 16 * k1, 16), v("ZB", k0, k1))
+        ops[-2]["early"], ops[-2]["lat"] = ZEARLY, FAR + 1000
+        zs = 0
+        for q, k0, k1 in COPIES:
+            if q == "V":
+                n = 16 * (k1 - k0)
+                cp(v("ZS", zs, zs + n, 16), v("ZB", k0, k1))
+                scan(v("ZX", 16 * k0, 16 * k1), v("KEEP", 0, n), v("ZS", zs, zs + n), OP.mult, OP.add)
+                zs += n
+            for m in range(16 * (q != "V")):
+                (act if q == "A" else gcp)(v("ZX", 16 * k0 + m, 16 * k1, 16), v("ZB", k0, k1))
         ts(v("HM"), v("H16"), 1.0, OP.add)
         if t:
             cp(ind(v("NW", A, A + AREA), v("FIX", 0, 3)), v("NB", CAP * (t - 1), CAP * t))
             numbers(A)
             put_course(t - 1)
         slots(t)
-        dist(CUTS, "H16", "ZX", "DF")
+        dist(OWN, "H16", "ZB", "ZX", "DF")
         asking()
         message("q", t, lender, asker, v("LSL", 8 * t, 8 * t + 4), v("LST"))
         hashes([("ZL", z, "WA", 256)], [("HL", 0, 256)])
@@ -522,19 +624,22 @@ def rank_program(g, core, T, topo):
         asker_slots()
         lst = v("LSL", 8 * t, 8 * t + 3)
         cp(v("H16L"), ind(v("HL"), lst))
-        cp(v("ZSL", 0, 768, 16), ind(v("ZL", z, z + WIN), lst))
-        scan(v("ZXL"), v("KEEP", 0, 768), v("ZSL"), OP.mult, OP.add)
+        n = 16 * max(k1 for k0, k1, bank in LENT if not bank)
+        cp(v("ZSL", 0, n, 16), ind(v("ZL", z, z + WIN), v("LSL", 8 * t, 8 * t + n // 256)))
+        scan(v("ZXL", 0, n), v("KEEP", 0, n), v("ZSL", 0, n), OP.mult, OP.add)
+        if n < 16 * CAP:
+            act(v("ZA"), ind(v("ZL", z, z + WIN), lst))
         ts(v("HML"), v("H16L"), 1.0, OP.add)
         act(v("U", DL, DL + CAP), v("AI", 0, CAP), scale=0.0)
-        dist([0, 32, 48], "H16L", "ZXL", "DFL")
+        dist(LENT, "H16L", "ZA", "ZXL", "DFL")
         choose(CAP, False, "HML", "DC2", "LEN")
         r0 = RETN * t
-        ts(v("RESP", 48, 51), v("CS", 15, CAP, 16), float(S), OP.is_ge, 256.0, OP.mult)
-        if last:
-            message("a", t, asker, lender, v("RETL", r0 + 48, r0 + RETN), v("RESP", 48, RETN))
-        else:
-            cp(v("RESP", 0, 48), ind(v("TW", 0, A0), v("LEN", 0, 3)))
-            message("a", t, asker, lender, v("RETL", r0, r0 + RETN), v("RESP"))
+        if not last:
+            ts(v("EL", 0, 3), v("LS", 15, CAP, 16), -1.0, OP.add)
+            act(v("REST"), ind(v("TW", 0, S), v("EL", 0, 3)))
+            message("t", t, asker, lender, v("RETL", r0, r0 + CAP), v("REST"))
+        ts(v("RESF", 0, 3), v("CS", 15, CAP, 16), float(S), OP.is_ge, 256.0, OP.mult)
+        message("a", t, asker, lender, v("RETL", r0 + CAP, r0 + RETN), v("RESF"))
         act(v("RESU"), ind(v("U", 0, A0), v("LEN", 0, 3)))
         message("u", t, asker, lender, v("UB", CAP * t, CAP * t + CAP), v("RESU"))
         cp(ind(v("U", 0, A0), v("LEN", 0, 3)), v("C255", 0, 48))
@@ -554,44 +659,9 @@ def rank_program(g, core, T, topo):
     put_course(RO - 1)
     dma("A", T.yu[:, S:S + RO * CAP], v("UB"))
 
-    n = len(ops)
-    nxt = [[] for _ in ops]
-    for i, o in enumerate(ops):
-        for j in o["pre"] | o["after"]:
-            nxt[j].append(i)
-
-    def gap(j, i):
-        return 0 if ops[i]["q"] == "N" or ops[j]["q"] == ops[i]["q"] == "P" else WAKE
-    tail = [0] * n
-    for i in range(n - 1, -1, -1):
-        tail[i] = ops[i]["dur"] + ops[i]["lat"] + max([gap(i, j) + tail[j] for j in nxt[i]] + [0])
-    left = [len(o["pre"] | o["after"]) for o in ops]
-    ready = {i: 0 for i in range(n) if not left[i]}
-    free = {q: 0 for q in "VAPGSN"}
-    used = {b: {} for b in _ps}
-    end = [0] * n
-    order = []
-
-    def begin(i):
-        o = ops[i]
-        return max([free[o["q"]], ready[i]] + [e + WAKE for b in o["banks"] for q, e in used[b].items() if q != o["q"]])
-    while ready:
-        start = {i: begin(i) for i in ready}
-        first = min(ready, key=lambda i: (start[i] + ops[i]["dur"], i))
-        q, by = ops[first]["q"], start[first] + ops[first]["dur"]
-        i = max((j for j in ready if ops[j]["q"] == q and (start[j] < by or j == first)), key=lambda j: (tail[j], -j))
-        o = ops[i]
-        if q != "N":
-            free[q] = start[i] + o["dur"]
-        end[i] = start[i] + o["dur"] + o["lat"]
-        for b in o["banks"]:
-            used[b][q] = end[i]
-        del ready[i]
-        order.append(i)
-        for j in nxt[i]:
-            left[j] -= 1
-            if not left[j]:
-                ready[j] = max(end[k] + gap(k, j) for k in ops[j]["pre"] | ops[j]["after"])
+    if "order" not in _once:
+        _once["order"] = issue_order(ops)
+    order = _once["order"]
 
     count = {"V": 0, "A": 0, "P": 0, "G": 0}
     know = {q: {} for q in Q}

from concourse.mybir import AluOpType as OP, ActivationFunctionType as AF

RO, CAP, L, S = 5, 48, 256, 2048
DL = S
A0 = S + 64
AREA = 560
WID = A0 + 2 * AREA
WIN = 272
RETN = 56
BIG = 4096.0
ROUND = 1.5 * 2.0 ** 34

_sb = {
    "U": (WID, "bfloat16"), "TW": (WID, "bfloat16"), "NW": (WID, "bfloat16"), "NH": (S, "bfloat16"),
    "C0L": (16, "int32"), "HWI": (2, "int32"), "KMI": (1, "int32"), "THI": (1, "int32"),
    "PIX": (1, "int32"), "PA_": (1, "int32"), "PG_": (1, "int32"), "PB_": (1, "int32"), "PC_": (1, "int32"), "PD_": (1, "int32"),
    "COL": (32, "float32"), "SELC": (16, "float32"),
    "GI": (128, "float32"), "YI": (144, "float32"), "AI": (256, "float32"),
    "BO": (128, "bfloat16"), "BO4": (128, "bfloat16"), "BON": (128, "bfloat16"), "IDB": (128, "bfloat16"), "SB": (144, "bfloat16"),
    "S16": (144, "bfloat16"), "SN": (144, "bfloat16"), "S0": (144, "bfloat16"), "S0N": (144, "bfloat16"), "S15": (144, "bfloat16"),
    "SR": (384, "bfloat16"), "SR2": (1024, "bfloat16"), "SEL2": (16, "float32"), "NN2": (32, "bfloat16"), "NZ2": (32, "float32"),
    "F2": (32, "bfloat16"), "EL": (4, "uint16"), "REST": (CAP, "bfloat16"), "RESF": (8, "bfloat16"), "PAM": (128, "bfloat16"), "PBM": (128, "bfloat16"), "HID": (128, "bfloat16"), "DM": (128, "bfloat16"),
    "SHM": (128, "bfloat16"), "TRI": (128, "bfloat16"), "ONE": (256, "bfloat16"), "NEG": (128, "bfloat16"), "E0": (128, "bfloat16"),
    "HALF": (128, "float16"), "M2": (256, "bfloat16"), "MB": (256, "bfloat16"), "R0": (256, "float32"), "RST": (256, "float32"),
    "KEEP": (1024, "bfloat16"), "CL0": (16, "float32"), "DC0": (16, "float32"), "DC1": (16, "float32"), "DC2": (16, "float32"),
    "FOUR": (16, "float32"), "IB": (16, "float32"), "SI": (16, "bfloat16"), "KC": (16, "float32"),
    "NB": (240, "bfloat16"), "C255": (256, "bfloat16"), "E8": (128, "float32"), "THF": (16, "float32"), "TH32": (1, "float32"),
    "THR": (1, "float32"), "WA": (144, "float16"), "WL": (144, "float16"), "WR": (144, "float16"), "WF": (2, "float32"), "WI": (2, "int32"),
    "KD": (16, "float16"), "KF": (1, "float32"), "KI1": (1, "int32"), "KW": (16, "int32"), "KW2": (16, "int32"), "TMPC": (128, "float32"),
    "PT": (32, "float32"), "PU": (32, "float32"), "JL": (16, "uint16"),
    "ZB": (256, "bfloat16"), "UVI": (32, "int32"), "UVM": (32, "int32"), "TT": (16, "int32"), "TSI": (256, "int32"),
    "TXF": (256, "float16"), "Y": (256, "float32"), "H16": (256, "uint16"), "HM": (256, "float16"),
    "HL": (WIN, "int32"), "H16L": (48, "uint16"), "HML": (48, "float16"),
    "ZS": (1024, "bfloat16"), "ZX": (4096, "bfloat16"), "DF": (4096, "bfloat16"), "KY": (256, "int32"),
    "ZSL": (768, "bfloat16"), "ZXL": (768, "bfloat16"), "DFL": (768, "bfloat16"),
    "PQ": (16, "bfloat16"), "XN": (32, "bfloat16"), "CUM": (WIN, "bfloat16"), "CNT": (4, "float32"), "LST": (4, "uint16"),
    "JUNK": (2816, "bfloat16"), "NID": (128, "bfloat16"), "Y1": (256, "float32"), "ZA": (48, "bfloat16"), "GA": (48, "bfloat16"), "GB": (48, "bfloat16"), "PIN": (1, "int32"), "PI2": (1, "int32"),
    "MC": (16, "int32"), "CODE": (32, "bfloat16"), "OH": (256, "float16"), "HO": (256, "float16"),
    "HR": (256, "float16"), "LS": (256, "float32"), "EI": (256, "bfloat16"), "EB": (1920, "bfloat16"), "EA": (768, "float32"),
    "CS": (256, "float32"), "LAY": (16, "uint16"), "LEN": (4, "uint16"),
    "CI": (16, "int32"), "CW": (16, "int32"), "CE": (32, "bfloat16"), "CFI": (32, "int32"), "F1": (32, "bfloat16"),
    "NN": (16, "bfloat16"), "NZ": (16, "float32"), "F0R": (WIN, "bfloat16"), "JC": (16, "float32"), "JN": (32, "float16"),
    "JF": (16, "float32"), "SLOT": (16, "uint16"), "FIX": (4, "uint16"), "CF": (80, "float32"),
    "ZL": (RO * WIN, "bfloat16"), "LSL": (RO * 8, "uint16"), "RESU": (CAP, "bfloat16"),
    "RETL": (RO * RETN, "bfloat16"), "UB": (240, "bfloat16"),
}
_ps = ("pA", "pB", "pS", "pD", "pC", "pH", "pN", "pX")
_place = {}
_fill = {}
for _k in _sb:
    if _sb[_k][0] <= 48:
        _d = _sb[_k][1]
        _place[_k] = ("pack_" + _d, _fill.get(_d, 0))
        _fill[_d] = _fill.get(_d, 0) + (_sb[_k][0] + 15) // 16 * 16
SCRATCH = {k: ("sbuf", [128, _sb[k][0]], _sb[k][1]) for k in _sb if k not in _place}
SCRATCH.update({"pack_" + k: ("sbuf", [128, _fill[k]], k) for k in _fill})
SCRATCH.update({k: ("psum", [128, 512], "float32") for k in _ps})
_bytes = {"bfloat16": 2, "float16": 2, "uint16": 2, "float32": 4, "int32": 4}
MSG = ("z", "q", "t", "a", "u")
SEMAPHORES = ["sV", "sA", "sP", "sG"] + ["d%d" % i for i in range(16)] + [e + m + str(t) for e in "lr" for m in MSG for t in range(RO)]
OWN = [(0, 32, None), (96, 128, None), (32, 64, "pC"), (128, 160, None), (64, 96, "pH"), (160, 192, None), (192, 224, None),
       (224, 240, None), (240, 256, None)]
LENT = [(0, 16, None), (32, 48, "pC"), (16, 32, None)]
COPIES = [("V", 0, 32), ("A", 96, 192), ("G", 192, 256)]
TURNS, STEPS = 3, (0, 200)
EARLY = 2000
ZEARLY = 6000
EIAT = 6
HCUT = 96
KV = 11
LEAST, WAKE, GATHER, SCATTER, FAR, NEAR = 64, 140, 1.5, 3.5, 2600, 1600


_once = {}


def issue_order(ops):
    n = len(ops)
    pre = [{j: ops[j]["lat"] + (0 if o["q"] == "N" or o["q"] == ops[j]["q"] == "P" else WAKE) for j in o["pre"] | o["after"]} for o in ops]
    nxt = [{} for _ in ops]
    for i in range(n):
        for j in pre[i]:
            nxt[j][i] = pre[i][j] + ops[j].get("early", 0)

    def place(seq, before, back):
        end = [0] * n
        line = {}
        for i in seq:
            o = ops[i]
            q, d = o["q"], o["dur"]
            t = max([end[j] + w for j, w in before[i].items()] + [o["lat"] if back else 0])
            lines = [(line.setdefault(q, []), 0)] * (q != "N") + [(line.setdefault((b, e), []), WAKE) for b in o["banks"] for e in "VAP" if e != q]
            moved = True
            while moved:
                moved = False
                for taken, w in lines:
                    k = seek(taken, t - w)
                    while k < len(taken) and taken[k][0] < t + d + w:
                        t, k, moved = taken[k][1] + w, k + 1, True
            for key in [q] * (q != "N") + [(b, q) for b in o["banks"]]:
                taken = line.setdefault(key, [])
                taken.insert(seek(taken, t), (t, t + d))
            end[i] = t + d
        return end

    def seek(taken, t):
        lo, hi = 0, len(taken)
        while lo < hi:
            mid = (lo + hi) // 2
            if taken[mid][1] > t:
                hi = mid
            else:
                lo = mid + 1
        return lo
    best = None
    for step in STEPS:
        key = [0] * n
        for i in range(n - 1, -1, -1):
            key[i] = ops[i]["dur"] + max([w + step * (ops[j]["q"] in "VA") + key[j] for j, w in nxt[i].items()] + [ops[i]["lat"]])
        for turn in range(TURNS):
            end = place(sorted(range(n), key=lambda i: (-key[i], i)), pre, False)
            total = max(end[i] + ops[i]["lat"] for i in range(n))
            if best is None or total < best[0]:
                best = (total, sorted(range(n), key=lambda i: (end[i] - ops[i]["dur"], end[i], i)), step, turn)
            key = place(sorted(range(n), key=lambda i: (-end[i], -i)), nxt, True)
    _once["best"] = (best[0], best[2], best[3])
    return best[1]


def rank_program(g, core, T, topo):
    rank = T.rank_of(core)
    if rank is None:
        return
    cores = list(T.cores)
    N = len(cores)
    Q = {"V": g.vector, "A": g.scalar, "P": g.tensor, "G": g, "S": g.sync}

    def v(b, c0=0, c1=None, st=1, p=128, rows=None):
        p = rows or p
        if b in _place:
            o = _place[b][1]
            return (_place[b][0], o + c0, o + (_sb[b][0] if c1 is None else c1), st, p)
        return (b, c0, (SCRATCH[b][1][1] if c1 is None else c1), st, p)

    def ind(w, o):
        return ("I", w, o)

    def ap(x):
        if not isinstance(x, tuple):
            return x
        if x[0] == "I":
            return ap(x[1]).indirect(ap(x[2]))
        b, c0, c1, st, p = x
        t = T[b]
        if isinstance(p, tuple):
            return t[p[0]:p[1]:p[2], c0:c1]
        if st == 1:
            return t[:, c0:c1] if p == 128 else t[0:p, c0:c1]
        return t[:, c0:c1:st] if p == 128 else t[0:p, c0:c1:st]

    def size(x):
        return 16 * size(x[2]) if x[0] == "I" else len(range(x[1], x[2], x[3]))

    def width(x):
        return _bytes[SCRATCH[x[1][0] if x[0] == "I" else x[0]][2]]

    def psum(b):
        return SCRATCH[b][0] == "psum"

    def cols(x, blocks):
        b, c0, c1, st, p = x
        if blocks:
            n = 16 // width(x)
            c0, c1, st = c0 // n * n, (c1 + n - 1) // n * n, 1
        if st == 1:
            return ((1 << (c1 - c0)) - 1) << c0
        return sum(1 << c for c in range(c0, c1, st))

    ops = []
    reads, writes, last_pe = {}, {}, {}

    def add(q, out, ins, f, dur, lat=0, own=None, after=()):
        rd, wr = [], []
        for x in ins:
            if isinstance(x, tuple):
                rd += [x[1], x[2]] if x[0] == "I" else [x]
        if isinstance(out, tuple):
            if out[0] == "I":
                wr.append(out[1])
                rd.append(out[2])
            else:
                wr.append(out)
        i = len(ops)
        pre = set()
        for x in rd:
            m = cols(x, own is not None)
            pre.update(j for mj, j in writes.get(x[0], []) if m & mj)
        for x in wr:
            b, m = x[0], cols(x, own is not None)
            pre.update(j for mj, j in writes.get(b, []) + reads.get(b, []) if m & mj)
            if q == "P":
                pre.update(last_pe.get(b, []))
                last_pe[b] = [i]
            if x[4] == 128 and out[0] != "I":
                writes[b] = [e for e in writes.get(b, []) if e[0] & ~m]
                reads[b] = [e for e in reads.get(b, []) if e[0] & ~m]
            elif out[0] == "I":
                writes[b] = [e for e in writes.get(b, []) if e[0] & ~m]
                reads[b] = [e for e in reads.get(b, []) if e[0] & ~m]
            writes.setdefault(b, []).append((m, i))
        for x in rd:
            reads.setdefault(x[0], []).append((cols(x, own is not None), i))
        ops.append({"q": q, "f": f, "dur": dur, "lat": lat, "pre": pre, "after": set(after), "own": own,
                    "banks": {x[0] for x in rd + wr if psum(x[0])}})
        return i

    def vlen(out, ins, two=False):
        full = [x for x in [out] + ins if isinstance(x, tuple) and size(x) == size(out)]
        if out[0] == "I":
            return 50 + SCATTER * size(out)
        if any(x[0] == "I" for x in full):
            return 50 + GATHER * size(out)
        r = 0.5 if all(width(x) == 2 for x in full) else 1.0
        return max(LEAST, size(out) * r * (2 if two and not any(psum(x[0]) for x in ins) else 1))

    def cp(out, in_):
        add("V", out, [in_], lambda: g.vector.tensor_copy(out=ap(out), in_=ap(in_)), vlen(out, [in_]))

    def tt(out, a, b, op):
        add("V", out, [a, b], lambda: g.vector.tensor_tensor(out=ap(out), in0=ap(a), in1=ap(b), op=op), vlen(out, [a, b], True))

    def ts(out, a, s1, op0, s2=None, op1=None):
        if op1 is None:
            add("V", out, [a, s1], lambda: g.vector.tensor_scalar(out=ap(out), in0=ap(a), scalar1=ap(s1), scalar2=None, op0=op0), vlen(out, [a]))
        else:
            add("V", out, [a, s1, s2], lambda: g.vector.tensor_scalar(out=ap(out), in0=ap(a), scalar1=ap(s1), scalar2=ap(s2), op0=op0, op1=op1),
                vlen(out, [a]))

    def scan(out, d0, d1, op0, op1, initial=0.0):
        add("V", out, [d0, d1], lambda: g.vector.tensor_tensor_scan(out=ap(out), data0=ap(d0), data1=ap(d1), initial=initial, op0=op0, op1=op1),
            vlen(out, [d0, d1]))

    def fill(out, c):
        add("V", out, [], lambda: g.vector.memset(ap(out), c), vlen(out, []))

    def act(out, in_, func=AF.Copy, scale=1.0, bias=0.0, total=None):
        n = size(out)
        if total is None:
            add("A", out, [in_, scale, bias], lambda: g.scalar.activation(out=ap(out), in_=ap(in_), func=func, bias=ap(bias), scale=ap(scale)),
                65 + GATHER * n if in_[0] == "I" else max(LEAST, n))
        else:
            add("A", total, [in_, scale, bias], lambda: g.scalar.activation(out=ap(out), in_=ap(in_), func=func, bias=ap(bias), scale=ap(scale),
                                                                            accum_out=ap(total)), max(LEAST, n) + 20)
            ops[-1]["pre"].update(dumps.get(out, []))
            dumps[out] = [len(ops) - 1]
    dumps = {}

    def gcp(out, in_):
        add("G", out, [in_], lambda: g.affine_select(ap(out), ap(in_), [[0, size(out)]], OP.is_ge, 0.0, 0, 0), 170 + 2 * size(out))

    def mm(out, lhsT, rhs, start=True, stop=True):
        add("P", out, [lhsT, rhs], lambda: g.tensor.matmul(ap(out), ap(lhsT), ap(rhs), start=start, stop=stop),
            max(min(64, size(lhsT)), size(rhs)) * (2 if width(rhs) == 4 else 0.5))

    def iota(out, pat, base=0, cm=0):
        if SCRATCH[out[0]][2] != "int32":
            add("G", out, [], lambda: g.iota(ap(out), pat, base, cm, allow_small_or_imprecise_dtypes=True), 130 + 2 * size(out))
        else:
            add("G", out, [], lambda: g.iota(ap(out), pat, base, cm), 130 + 2 * size(out))

    dmas = []

    def dma(q, out, in_, lat=NEAR, after=()):
        s = "d%d" % len(dmas)
        dmas.append(s)
        return add(q, out, [in_], lambda: Q[q].dma_start(out=ap(out), in_=ap(in_)).then_inc(T.sem[s], 16), 50, lat, (s, 16), after)

    def engs(src, dst):
        return topo.engines(src, dst)[:8]

    far = []

    def message(m, t, dst, src, out, in_):
        mask = sum(1 << e for e in engs(core, dst))
        rid, pid = topo.addr(dst, core)
        ls, rs = ("l%s%d" % (m, t), len(engs(core, dst))), ("r%s%d" % (m, t), len(engs(src, core)))
        far.extend([ls, rs])
        i = add("G", None, [in_], lambda: g.remote_dma(ap(out), ap(in_), T.sem[rs[0]], T.sem[ls[0]], pid, rid, mask), 300, FAR, ls)
        add("N", out, [], None, 0, 0, rs, [i])

    dma("S", v("C0L"), T.c0[:])
    d_tp = dma("S", v("TW", 0, S), T.tp[:], 2 * NEAR)
    dma("A", v("HWI"), T.hw[:])
    dma("A", v("KMI"), T.km[:])
    dma("A", v("THI", p=8), T.th[:])
    dma("S", v("U", 0, S), T.us[:], 3 * NEAR)
    iota(v("PIX"), [[0, 1]], 0, 1)
    iota(v("GI"), [[1, 8], [0, 16]])
    iota(v("AI"), [[0, 16], [1, 16]])
    iota(v("YI"), [[1, 144]])
    iota(v("CL0"), [[16, 16]])
    iota(v("KC", 0, 12), [[31, 12]], 18)
    iota(v("KC", 12, 16), [[11, 4]], 386)
    for h in (0, 1):
        iota(v("NW", 1024 * h, 1024 * h + 1024), [[0, 64], [1, 16]])
        iota(v("NH", 1024 * h, 1024 * h + 1024), [[1, 64], [0, 16]], 64 * h)
    dma("S", v("NW", 0, S, rows=(0, 128, 16)), v("NH", 0, S, rows=(0, 8, 1)))
    iota(v("NB"), [[0, 15], [1, 16]])
    iota(v("NH", 0, 240), [[1, 15], [0, 16]], 128)
    dma("S", v("NB", rows=(0, 128, 16)), v("NH", 0, 240, rows=(0, 8, 1)))
    PIX, GI, YI, AI16 = v("PIX"), v("GI"), v("YI", 0, 128), v("AI", 0, 16)

    def col(i):
        return v("COL", i, i + 1)
    ts(v("PA_"), PIX, 15, OP.bitwise_and)
    ts(v("PG_"), PIX, 4, OP.arith_shift_right)
    ts(v("PB_"), PIX, 4, OP.arith_shift_right, 1, OP.bitwise_and)
    cp(col(0), v("PA_"))
    cp(col(1), v("PG_"))
    cp(col(3), PIX)
    cp(col(6), v("PB_"))
    ts(col(5), v("PB_"), -1.0, OP.mult, 1.0, OP.add)
    ts(col(2), v("PG_"), 16.0, OP.mult, 15.0, OP.add)
    ts(col(4), v("PA_"), 2.0, OP.mult)
    ts(col(7), v("PA_"), 8.0, OP.is_ge)
    ts(col(8), v("PA_"), 8.0, OP.is_lt)
    ts(col(9), PIX, -8.0, OP.add)
    ts(col(10), PIX, 8.0, OP.add)
    ts(col(11), v("PA_"), 0.0, OP.is_equal)
    ts(col(12), v("PA_"), 0.0, OP.is_equal, -1.0, OP.mult)
    ts(col(14), v("PA_"), 16.0, OP.mult)
    ts(col(15), v("PA_"), 15.0, OP.is_equal, -0.5, OP.mult)
    ts(col(16), v("PA_"), 15.0, OP.is_lt, -0.5, OP.mult)
    ts(col(17), PIX, 1.0, OP.add)
    ts(col(18), v("PA_"), 2.0, OP.is_lt)
    ts(v("PC_"), PIX, 1, OP.bitwise_and)
    ts(col(19), v("PC_"), 0.0, OP.is_equal)
    cp(col(20), v("PC_"))
    ts(col(13), col(11), 15.0, OP.mult, col(18), OP.add)
    ts(v("BO"), GI, col(1), OP.is_equal)
    ts(v("SELC"), AI16, col(0), OP.is_equal)
    ts(v("SB"), v("YI"), col(2), OP.is_equal)
    ts(v("IDB"), YI, col(3), OP.is_equal)
    ts(v("PAM"), YI, col(9), OP.is_equal, col(7), OP.mult)
    ts(v("PBM"), YI, col(10), OP.is_equal, col(8), OP.mult)
    for j in range(4):
        act(v("KEEP", 256 * j, 256 * j + 256), v("AI"), AF.Sign)
    K256 = v("KEEP", 0, 256)

    def const(out, c):
        for j in range(out[1], out[2], 256):
            n = min(256, out[2] - j)
            act((out[0], j, j + n, 1, 128), v("AI", 0, n), scale=0.0, bias=c)
    const(v("ONE"), 1.0)
    const(v("NEG"), -1.0)
    fill(v("ZS"), 0.0)
    fill(v("ZSL"), 0.0)
    const(v("R0"), -1048576.0)
    const(v("C255"), 255.0)
    const(v("CUM", 0, 1), 0.0)
    const(v("CUM", 257, WIN), 0.0)
    const(v("F0R", 256, WIN), 256.0)
    const(v("CE", 0, 1), 0.0)
    const(v("CNT", 3, 4), 0.0)
    const(v("RESF", 3, 8), 0.0)
    for b in ("U", "TW", "NW"):
        const(v(b, S, A0), 0.0)
        fill(v(b, A0 + (0 if b == "U" else L), WID), 0.0)
    for t in range(RO):
        const(v("ZL", WIN * t + 256, WIN * t + WIN), 1024.0)
    act(v("RST"), K256, scale=-1048576.0, bias=1048576.0)
    act(v("M2"), v("AI"), scale=2.0)
    act(v("S16"), v("SB"), scale=32.0)
    act(v("SN"), v("SB"), scale=col(13))
    act(v("S0"), v("SB"), scale=col(11))
    act(v("S0N"), v("SB"), scale=col(12))
    act(v("S15"), v("SB"), scale=col(15))
    act(v("HID"), v("IDB"), scale=0.5)
    act(v("NID"), v("IDB"), scale=-1.0)
    act(v("BO4"), v("BO"), scale=BIG)
    act(v("BON"), v("BO"), scale=-BIG)
    act(v("E0"), v("ONE", 0, 128), scale=col(11))
    tt(v("SEL2", 0, 8), v("SELC", 0, 16, 2), v("SELC", 1, 16, 2), OP.add)
    for r in range(3):
        act(v("SR", 128 * r, 128 * r + 128), v("BO"), scale=v("SELC", r, r + 1))
    for r in range(8):
        act(v("SR2", 128 * r, 128 * r + 128), v("BO"), scale=v("SEL2", r, r + 1))
    fill(v("HL", 256, WIN), 0)
    fill(v("TSI"), 0)
    ts(v("HALF", p=32), v("GI", p=32), 0.0, OP.mult, -1023.5, OP.add)
    ts(v("JN", 0, 1), PIX, 0.0, OP.mult, -2.0, OP.add)
    for h in (0, 1):
        ts(v("PT", 16 * h, 16 * h + 16), v("C0L"), col(5 + h), OP.mult)
    add("V", v("PU"), [v("PT")], lambda: g.vector.transpose(out=ap(v("PU")), in_=ap(v("PT"))), LEAST)
    tt(v("JL"), v("PU", 0, 16), v("PU", 16, 32), OP.add)
    cp(v("TW", A0, A0 + L), ind(v("TW", 0, S), v("JL")))
    act(v("NW", A0, A0 + L), ind(v("NW", 0, S), v("JL")))
    ts(v("WI"), v("HWI"), 2047, OP.bitwise_and)
    cp(v("WF"), v("WI"))
    for i in (0, 1):
        ts(v("WA", 8 * i, 8 * i + 8), v("GI", 0, 128, 16), col(1), OP.is_equal, v("WF", i, i + 1), OP.mult)
    ts(v("KI1"), v("KMI"), 2047, OP.bitwise_and)
    cp(v("KF"), v("KI1"))
    ts(v("KD"), AI16, col(0), OP.is_equal, v("KF"), OP.mult)
    mm(v("pX", 0, 16), v("BO"), v("KD"))
    ts(v("KW"), v("pX", 0, 16), v("WF", 0, 1), OP.mult)
    ts(v("KW2"), v("KW"), 2047, OP.bitwise_and)
    for j in range(8):
        tt(v("WA", 16 + 16 * j, 32 + 16 * j), v("KW2"), v("BO", 16 * j, 16 * j + 16), OP.mult)
    mm(v("pN", 0, 144), v("PBM"), v("WA"))
    mm(v("pC", 0, 144), v("PAM"), v("WA"))
    cp(v("WL"), v("pN", 0, 144))
    cp(v("WR"), v("pC", 0, 144))
    cp(v("THF", 0, 1, p=8), v("THI", p=8))
    ts(v("E8", p=8), v("GI", p=8), v("COL", 3, 4, p=8), OP.is_equal)
    mm(v("pX", 16, 17), v("E8", p=8), v("THF", 0, 1, p=8))
    ts(v("TH32"), v("pX", 16, 17), 32.0, OP.mult, -1.0, OP.add)
    cp(v("THR"), v("TH32"))
    ts(v("TMPC"), v("AI", 0, 128), col(0), OP.is_gt)
    tt(v("TRI"), v("TMPC"), v("BO"), OP.mult)
    ts(v("SHM"), YI, col(17), OP.is_equal, col(16), OP.mult)
    tt(v("DM"), v("SHM"), v("HID"), OP.add)
    ts(v("MB"), v("AI"), col(0), OP.not_equal, 2 * BIG, OP.mult)
    ts(v("FOUR"), AI16, col(14), OP.add, 254.0, OP.is_equal)
    ts(v("FOUR"), v("FOUR"), 1600.0, OP.mult, 4.0, OP.add)
    ts(v("SI"), v("CL0"), col(0), OP.add)
    ts(v("IB"), v("CL0"), col(0), OP.add, 0.5, OP.add)
    ts(v("DC0"), v("CL0"), col(0), OP.add, float(A0), OP.add)
    ts(v("DC1"), v("CL0"), col(0), OP.add, float(A0 + AREA), OP.add)
    ts(v("DC2"), v("CL0"), col(0), OP.add, float(DL), OP.add)

    def sel(b, r):
        return v(b, 15 - r, 143 - r)

    def spread(out, c0, x):
        for r in range(8):
            mm(v(out, c0 + 32 * r, c0 + 32 * r + 32), v("SR2", 128 * r, 128 * r + 128), x)

    def hashes(terms, outs):
        for b in (0, 1):
            for i in (0, 1):
                for j, (z, zc, w, n) in enumerate(terms):
                    mm(v("pB", 16 * i + 8 * b, 16 * i + 8 * b + 8), v(z, zc + 128 * b, zc + 128 * b + 128), v(w, 8 * i, 8 * i + 8), j == 0, j == len(terms) - 1)
        mm(v("pD", 256, 512), v("HALF", p=1), v("ONE", p=1), True, False)
        for bank, h in (("pD", 256), ("pS", 0)):
            for j, (z, zc, w, n) in enumerate(terms):
                mm(v(bank, h, h + n), v(w, 16, 144), v(z, zc, zc + n), h + j == 0, False)
        cp(v("UVI"), v("pB", 0, 32))
        ts(v("UVM"), v("UVI"), 2047, OP.bitwise_and)
        tt(v("TT"), v("UVM", 0, 16), v("UVM", 16, 32), OP.mult)
        ts(v("TSI", 0, 256, 16), v("TT"), 5, OP.arith_shift_right, 2047, OP.bitwise_and)
        for b in range(0, 256, 256 // len(terms)):
            e = b + 256 // len(terms)
            scan(v("TXF", b, e), v("KEEP", b, e), v("TSI", b, e), OP.mult, OP.add)
        for b in (0, 1):
            for bank, h in (("pD", 256), ("pS", 0)):
                mm(v(bank, h + 128 * b, h + 128 * b + 128), v("TXF", 128 * b, 128 * b + 128), v("IDB"), False, b == 1)
        for out, c0, c1 in outs:
            if len(terms) > 1:
                ts(v("Y", c0, c1), v("pD", 256 + c0, 256 + c1), ROUND, OP.add, -ROUND, OP.add)
            else:
                act(v("Y1", c0, c1), v("pD", 256 + c0, 256 + c1), bias=ROUND)
                act(v("Y", c0, c1), v("Y1", c0, c1), bias=-ROUND)
            tt(v(out, c0, c1), v("pS", c0, c1), v("Y", c0, c1), OP.subtract)

    def dist(pieces, h, z, zx, df):
        mm(v("pD", 0, 256), v("ONE", 0, 128, p=1), v("M2", p=1), True, False)
        for k0, k1, bank in pieces:
            x, stones = v(df, 16 * k0, 16 * k1), ind(v("U", 0, S), v(h, k0, k1))
            if bank:
                n = 16 * (k1 - k0)
                for m in range(16):
                    mm(v(bank, m, n, 16), v("NID"), v(z, k0, k1), m == 0, False)
                act(x, stones)
                mm(v(bank, 0, n), v("IDB"), x, False, True)
                act(x, v(bank, 0, n), AF.Abs)
            else:
                tt(x, stones, v(zx, 16 * k0, 16 * k1), OP.subtract)
                act(x, x, AF.Abs)
            for r in range(k0 // 16, k1 // 16):
                mm(v("pD", 0, 256), sel("S16", r), v(df, 256 * r, 256 * r + 256), False, k0 == pieces[-1][0] and r == k1 // 16 - 1)
        scan(v("KY"), v("R0"), v("pD", 0, 256), OP.max, OP.min, -1048576.0)

    KEY = v("KY", 15, 256, 16)

    def choose(n, own, hm, dc, lst):
        k = n // 16
        ts(v("MC"), KEY, 31, OP.bitwise_and)
        if own:
            for j in (0, 16):
                tt(v("CODE", j, j + 16), v("MC"), v("NZ2", j, j + 16), OP.min)
            spread("pC", 0, v("CODE"))
        else:
            cp(v("CODE", 0, 16), v("MC"))
            for r in range(k):
                mm(v("pC", 16 * r, 16 * r + 16), v("SR", 128 * r, 128 * r + 128), v("CODE", 0, 16))
        ts(v("OH", 0, n), v("pC", 0, n), col(4), OP.is_equal)
        tt(v("HO", 0, n), v("OH", 0, n), v(hm, 0, n), OP.mult)
        h1, h2, cnt = v("pH", 0, n), v("pC", 256, 256 + n), v("pN", 0, n)
        mm(h2, v("IDB"), v("MB", 0, n), True, False)
        mm(h2, v("BO"), v("HO", 0, n), False, True)
        mm(h1, v("BO"), v("HO", 0, n))
        mm(cnt, v("IDB"), v("MB", 0, n), True, False)
        mm(cnt, v("NEG", p=1), v("ONE", 0, n, p=1), False, False)
        mm(cnt, v("BON"), v("OH", 0, n), False, False)
        mm(cnt, v("BO"), v("HO", 0, n), False, False)
        scan(v("LS", 0, n), v("RST", 0, n), h2, OP.add, OP.min)
        if own:
            cp(v("HR"), h1)
        tt(v("EI", 0, n), h1, v("LS", 0, n), OP.is_equal)
        kv = min(KV, k - 1)
        o = [0]
        for c in range(k - 1):
            o.append(o[c] + n - 16 * (c + 1))
        for c in range(kv, k - 1):
            act(v("EA", o[c] - o[kv], o[c + 1] - o[kv]), v("pH", 16 * (c + 1), n), AF.Abs, -1.0, v("LS", 16 * c + 15, 16 * c + 16))
        if kv < k - 1:
            act(v("EB", o[kv], o[k - 1]), v("EA", 0, o[k - 1] - o[kv]), AF.Relu, -1.0, 1.0)
        for c in range(k - 1):
            if c < kv:
                ts(v("EB", o[c], o[c + 1]), v("HR" if own else "pH", 16 * (c + 1), n), v("LS", 16 * c + 15, 16 * c + 16), OP.is_equal)
            if c == min(EIAT, k - 2):
                mm(cnt, v("BO4"), v("EI", 0, n), False, False)
            mm(v("pN", 16 * (c + 1), n), v("BO4"), v("EB", o[c], o[c + 1]), False, c == k - 2)
        scan(v("CS", 0, n), v("RST", 0, n), cnt, OP.add, OP.min)
        tt(v(lst, 0, k), v("CS", 15, n, 16), v(dc, 0, k), OP.min)

    def numbers(A):
        for r in range(16):
            mm(v("pX", 0, 16), sel("SN", r), v("NW", A + 16 * r, A + 16 * r + 16), r == 0, r == 15)

    def put_course(t):
        act(v("CF", 16 * t, 16 * t + 16), v("pX", 0, 16))
        dma("S", T.yc[:, 256 * t:256 * t + 256], v("CF", 16 * t, 16 * t + 16))

    def slots(t):
        if t:
            cp(v("CI"), v("pX", 0, 16))
        ts(v("CW"), v("CI") if t else v("C0L"), 3, OP.bitwise_and)
        scan(v("CE", 1, 17), v("CW"), v("FOUR"), OP.add, OP.add)
        mm(v("pX", 16, 17), v("TRI"), v("CE", 16, 17))
        ts(v("CFI", 0, 17), v("CE", 0, 17), v("pX", 16, 17), OP.add, 0.2, OP.mult)
        ts(v("F1", 0, 17), v("CFI", 0, 17), 256.0, OP.min)
        tt(v("NN"), v("F1", 1, 17), v("F1", 0, 16), OP.subtract)
        ops[-1]["early"] = EARLY
        for j in (0, 1):
            x = (16 * j, 16 * j + 16)
            ts(v("NN2", *x), v("NN"), col(19 + j), OP.mult)
            act(v("F2", *x), v("F1", 0, 16), scale=col(19 + j))
            ts(v("NZ2", *x), v("NN2", *x), 32.0, OP.mult, col(19 + j), OP.subtract)
        spread("pA", 256, v("F2"))
        act(v("F0R", 0, 256), v("pA", 256, 512))
        for k in range(16):
            lo, hi = 11 * k, min(L, 20 * k + 20)
            act(v("JUNK", 128 * k, 128 * k + hi - lo), v("F0R", lo, hi), AF.Sign, -1.0, v("IB", k, k + 1), v("JC", k, k + 1))
        tt(v("JN", 1, 17), v("JC"), v("KC"), OP.add)
        mm(v("pX", 32, 48), v("DM"), v("JN", 1, 17), True, False)
        mm(v("pX", 32, 48), sel("S15", 0), v("JN", 0, 16), False, True)
        mm(v("pX", 48, 64), v("HID"), v("JN", 1, 17))
        ts(v("JF"), v("pX", 32, 48), 0.5, OP.is_ge, 256.0, OP.mult)
        tt(v("SLOT"), v("pX", 48, 64), v("JF"), OP.add)

    def asking():
        ts(v("PQ"), KEY, v("THR"), OP.is_ge)
        for j in (0, 16):
            tt(v("XN", j, j + 16), v("PQ"), v("NN2", j, j + 16), OP.mult)
        spread("pH", 256, v("XN"))
        scan(v("CUM", 1, 257), v("ONE"), v("pH", 256, 512), OP.mult, OP.add)
        for k in range(3):
            act(v("JUNK", 2048 + 256 * k, 2304 + 256 * k), v("CUM", 1, 257), AF.Sign, -1.0, v("IB", k, k + 1), v("CNT", k, k + 1))
        ts(v("LST"), v("CNT"), 0.5, OP.mult, 128.0, OP.add)

    def asker_slots():
        act(v("GA"), ind(v("F0R"), v("LST", 0, 3)))
        act(v("GB"), ind(v("CUM"), v("LST", 0, 3)))
        mm(v("pX", 64, 67), v("IDB"), v("SI", 0, 3), True, False)
        for b, x in (("S0", "GA"), ("S0N", "GB")):
            for p in range(16):
                mm(v("pX", 64, 67), sel(b, p), v(x, p, CAP, 16), False, b == "S0N" and p == 15)

    def bound():
        act(v("R0", 0, 256, 16), AI16, AF.Identity, 0.0, v("THR"))

    bound()
    for t in range(RO):
        A = A0 + AREA * (t % 2)
        B = A0 + AREA * (1 - t % 2)
        lender = cores[(rank + 1 + t % (N - 1)) % N]
        asker = cores[(rank - 1 - t % (N - 1)) % N]
        last = t == RO - 1
        hashes([("TW", A, "WL", 256), ("TW", A + 1, "WR", 256)], [("H16", 0, HCUT), ("H16", HCUT, 256)])
        mm(v("pA", 0, 256), v("PAM"), v("TW", A, A + L), True, False)
        mm(v("pA", 0, 256), v("PBM"), v("TW", A + 1, A + L + 1), False, True)
        act(v("ZB"), v("pA", 0, 256))
        z = WIN * t
        message("z", t, lender, asker, v("ZL", z, z + 256), v("ZB"))
        ops[-2]["early"], ops[-2]["lat"] = ZEARLY, FAR + 1000
        zs = 0
        for q, k0, k1 in COPIES:
            if q == "V":
                n = 16 * (k1 - k0)
                cp(v("ZS", zs, zs + n, 16), v("ZB", k0, k1))
                scan(v("ZX", 16 * k0, 16 * k1), v("KEEP", 0, n), v("ZS", zs, zs + n), OP.mult, OP.add)
                zs += n
            for m in range(16 * (q != "V")):
                (act if q == "A" else gcp)(v("ZX", 16 * k0 + m, 16 * k1, 16), v("ZB", k0, k1))
        ts(v("HM"), v("H16"), 1.0, OP.add)
        if t:
            cp(ind(v("NW", A, A + AREA), v("FIX", 0, 3)), v("NB", CAP * (t - 1), CAP * t))
            numbers(A)
            put_course(t - 1)
        slots(t)
        dist(OWN, "H16", "ZB", "ZX", "DF")
        asking()
        message("q", t, lender, asker, v("LSL", 8 * t, 8 * t + 4), v("LST"))
        hashes([("ZL", z, "WA", 256)], [("HL", 0, 256)])
        choose(256, True, "HM", "DC%d" % (t % 2), "LAY")
        cp(ind(v("U"), v("LAY")), v("C255"))
        if not last:
            act(v("TW", A + L, A + 2 * L), ind(v("TW", 0, A + L), v("LAY")))
            act(v("TW", B, B + L), ind(v("TW", A, A + 2 * L), v("SLOT")))
        act(v("NW", A + L, A + 2 * L), ind(v("NW", 0, A + L), v("LAY")))
        act(v("NW", B, B + L), ind(v("NW", A, A + 2 * L), v("SLOT")))
        asker_slots()
        lst = v("LSL", 8 * t, 8 * t + 3)
        cp(v("H16L"), ind(v("HL"), lst))
        n = 16 * max(k1 for k0, k1, bank in LENT if not bank)
        cp(v("ZSL", 0, n, 16), ind(v("ZL", z, z + WIN), v("LSL", 8 * t, 8 * t + n // 256)))
        scan(v("ZXL", 0, n), v("KEEP", 0, n), v("ZSL", 0, n), OP.mult, OP.add)
        if n < 16 * CAP:
            act(v("ZA"), ind(v("ZL", z, z + WIN), lst))
        ts(v("HML"), v("H16L"), 1.0, OP.add)
        act(v("U", DL, DL + CAP), v("AI", 0, CAP), scale=0.0)
        dist(LENT, "H16L", "ZA", "ZXL", "DFL")
        choose(CAP, False, "HML", "DC2", "LEN")
        r0 = RETN * t
        if not last:
            ts(v("EL", 0, 3), v("LS", 15, CAP, 16), -1.0, OP.add)
            act(v("REST"), ind(v("TW", 0, S), v("EL", 0, 3)))
            message("t", t, asker, lender, v("RETL", r0, r0 + CAP), v("REST"))
        ts(v("RESF", 0, 3), v("CS", 15, CAP, 16), float(S), OP.is_ge, 256.0, OP.mult)
        message("a", t, asker, lender, v("RETL", r0 + CAP, r0 + RETN), v("RESF"))
        act(v("RESU"), ind(v("U", 0, A0), v("LEN", 0, 3)))
        message("u", t, asker, lender, v("UB", CAP * t, CAP * t + CAP), v("RESU"))
        cp(ind(v("U", 0, A0), v("LEN", 0, 3)), v("C255", 0, 48))
        if not last:
            mm(v("pX", 18, 19), v("E0"), v("CUM", 256, 257))
            cp(v("PIN"), v("pX", 18, 19))
            ts(v("PI2"), v("PIN"), 63, OP.bitwise_and)
            ts(v("THR"), v("PI2"), 32.0, OP.mult, v("TH32"), OP.add)
            bound()
        tt(v("FIX", 0, 3), v("pX", 64, 67), v("RETL", r0 + 48, r0 + 51), OP.add)
        if not last:
            cp(ind(v("TW", B, B + AREA), v("FIX", 0, 3)), v("RETL", r0, r0 + 48))
    dma("S", T.yu[:, 0:S], v("U", 0, S), 3 * NEAR)
    B = A0 + AREA * (RO % 2)
    cp(ind(v("NW", B, B + AREA), v("FIX", 0, 3)), v("NB", CAP * (RO - 1), CAP * RO))
    numbers(B)
    put_course(RO - 1)
    dma("A", T.yu[:, S:S + RO * CAP], v("UB"))

    if "order" not in _once:
        _once["order"] = issue_order(ops)
    order = _once["order"]

    count = {"V": 0, "A": 0, "P": 0, "G": 0}
    know = {q: {} for q in Q}
    token, snap = {}, {}
    touched = {b: {} for b in _ps}
    for i in order:
        o = ops[i]
        q = o["q"]
        if q == "N":
            token[i] = o["own"]
            continue
        deps = [token[j] for j in o["pre"] if not ops[j]["q"] == q == "P"]
        deps += [tk for b in o["banks"] for e, tk in touched[b].items() if e != q]
        want = {}
        for s, val in deps:
            want[s] = max(want.get(s, 0), val)
        k = know[q]
        for s in sorted(want, key=lambda s: -len(snap.get((s, want[s]), ()))):
            if k.get(s, 0) < want[s]:
                Q[q].wait_ge(T.sem[s], want[s])
                k[s] = want[s]
                for s2, v2 in snap.get((s, want[s]), {}).items():
                    k[s2] = max(k.get(s2, 0), v2)
        if o["own"]:
            o["f"]()
            token[i] = o["own"]
        else:
            count[q] += 1
            o["f"]().then_inc(T.sem["s" + q], 1)
            token[i] = ("s" + q, count[q])
        snap[token[i]] = dict(k)
        for b in o["banks"]:
            touched[b][q] = token[i]
    for q in count:
        g.wait_ge(T.sem["s" + q], count[q])
    for s in dmas:
        g.sync.wait_ge(T.sem[s], 16)
    for s, val in far:
        g.wait_ge(T.sem[s], val)
